import numpy as np
import ml_dtypes


def mxq(x, axis, fmt="e4m3"):
    dtype, down = {"e4m3": (ml_dtypes.float8_e4m3fn, 7), "e5m2": (ml_dtypes.float8_e5m2, 14)}[fmt]
    v = np.moveaxis(np.asarray(x, np.float32).astype(ml_dtypes.bfloat16).astype(np.float64), axis, -1)
    blocks = v.reshape(v.shape[:-1] + (-1, 32))
    amax = np.abs(blocks).max(-1, keepdims=True)
    byte = np.maximum(np.where(amax > 0, np.frexp(amax)[1] - 1 + 127, 0) - down, 1)
    scale = np.exp2(byte - 127.0)
    codes = (blocks / scale).astype(np.float32).astype(dtype).astype(np.float64)
    return np.moveaxis((codes * scale).reshape(v.shape), -1, axis)


WIDE = False


def mx_kscale(k):
    if not WIDE:
        return np.ones(k)
    levels = np.array([10, -10, 5, -5, 0])
    if k % 512:
        return np.exp2(np.random.permutation(np.resize(levels, k // 32))).repeat(32)
    a = np.empty((k // 512, 16))
    for p in range(k // 512):
        a[p, :8] = np.random.permutation(np.resize(levels, 8))
        for g in range(8):
            far = levels[np.abs(levels - a[p, g]) >= 10]
            a[p, g + 8] = far[np.random.randint(len(far))]
    return np.exp2(a.ravel()).repeat(32)


def f64(x):
    return np.asarray(x).astype(np.float64)


def striped(idx):
    return np.tile(idx.reshape(-1, 16).T, (8, 1)).astype(np.uint16)


def unstriped(offs):
    return offs[:16].T.reshape(-1).astype(np.int64)


E2M1 = np.array([0.0, 0.5, 1.0, 1.5, 2.0, 3.0, 4.0, 6.0, -0.0, -0.5, -1.0, -1.5, -2.0, -3.0, -4.0, -6.0])


def pack_weight(w, fmt):
    k, n = w.shape
    w = f64(np.asarray(w, np.float32).astype(ml_dtypes.bfloat16)).reshape(k // 32, 32, n)
    amax = np.abs(w).max(1)
    if fmt == "e4m3":
        byte = np.frexp(amax)[1] - 1 + 127 - 7
    else:
        mant, ex = np.frexp(amax / 6.0)
        byte = np.where(mant > 0.5, ex, ex - 1) + 127
    byte = np.clip(np.where(amax > 0, byte, 1), 1, 254)
    scaled = (w * np.exp2(127.0 - byte)[:, None, :]).reshape(k, n).astype(np.float32)
    by_word = np.ascontiguousarray(scaled.reshape(k // 512, 128, 4, n).transpose(0, 1, 3, 2))
    if fmt == "e4m3":
        words = by_word.astype(ml_dtypes.float8_e4m3fn).view(np.uint8)
    else:
        c = by_word.astype(ml_dtypes.float4_e2m1fn).view(np.uint8) & 0xF
        words = (c[..., 0::2] | (c[..., 1::2] << 4)).reshape(k // 512, 128, 2 * n)
    return np.ascontiguousarray(words), np.ascontiguousarray(byte.astype(np.uint8).reshape(k // 512, 16, n))


def unpack_weight(words, scales, fmt):
    g, _, n = scales.shape
    words = np.ascontiguousarray(words).reshape(g, 128, n, -1)
    if fmt == "e4m3":
        vals = words.view(ml_dtypes.float8_e4m3fn).astype(np.float64)
    else:
        nib = np.empty((g, 128, n, 4), np.uint8)
        nib[..., 0::2] = words & 0xF
        nib[..., 1::2] = words >> 4
        vals = E2M1[nib]
    vals = vals * np.repeat(np.exp2(scales.astype(np.float64) - 127.0), 8, axis=1)[..., None]
    return vals.transpose(0, 1, 3, 2).reshape(g * 512, n)


def silu(v):
    return v / (1.0 + np.exp(-np.maximum(v, -700.0)))


K, T, E, B, H, N = 512, 512, 8, 4, 512, 256


def setup_inputs():
    n = np.random.standard_normal
    s = mx_kscale(K)
    u = mx_kscale(H)
    slot_token = np.random.permutation(T)[:128 * B]
    block = np.sort(np.random.randint(E, size=B))
    x = pack_weight(n((K, T)) * s[:, None], "e4m3")
    w1 = pack_weight(n((K, E * H)) / np.sqrt(K) / s[:, None] * np.tile(u, E), "e4m3")
    w2 = pack_weight(n((H, E * N)) / np.sqrt(H) / u[:, None], "e4m3")
    return {
        "x_words": x[0],
        "x_scales": x[1],
        "w1_words": w1[0],
        "w1_scales": w1[1],
        "w2_words": w2[0],
        "w2_scales": w2[1],
        "gate": (np.tile(np.random.uniform(0.2, 1.0, 128 * B), (128, 1))).astype(np.float32),
        "offs": striped(slot_token),
        "offs2": striped((block[:, None] * H + np.arange(H)).reshape(-1)),
        "offs3": striped((block[:, None] * N + np.arange(N)).reshape(-1)),
    }


def reference(x_words, x_scales, w1_words, w1_scales, w2_words, w2_scales, gate, offs, offs2, offs3):
    idx, idx2, idx3 = unstriped(offs), unstriped(offs2), unstriped(offs3)
    xq = unpack_weight(x_words, x_scales, "e4m3")[:, idx]
    w1 = unpack_weight(w1_words, w1_scales, "e4m3")[:, idx2]
    w2 = unpack_weight(w2_words, w2_scales, "e4m3")[:, idx3]
    h = np.concatenate([w1[:, m * H:(m + 1) * H].T @ xq[:, 128 * m:128 * m + 128] for m in range(B)], axis=1)
    hq = mxq(silu(h), 0, "e4m3")
    y = np.concatenate([w2[:, m * N:(m + 1) * N].T @ hq[:, 128 * m:128 * m + 128] for m in range(B)], axis=1)
    out = np.zeros((N, T))
    out[:, idx] = f64(gate[:1]) * y
    return out

@@ -1,0 +1,141 @@
+from contextlib import ExitStack
+
+import concourse.mybir as mybir
+from concourse.masks import make_identity
+
+K, T, E, B, H, N = 512, 512, 8, 4, 512, 256
+FLOPS = 2 * 128 * B * (K * H + H * N)
+
+F32 = mybir.dt.float32
+BF16 = mybir.dt.bfloat16
+I32 = mybir.dt.int32
+U32 = mybir.dt.uint32
+U16 = mybir.dt.uint16
+U8 = mybir.dt.uint8
+FP8X4 = mybir.dt.float8_e4m3fn_x4
+P = 128
+S = 128
+
+
+def tile_moe_dyn_silu_kernel(
+    tc, x_words, x_scales, w1_words, w1_scales, w2_words, w2_scales, gate, offs, offs2, offs3, out
+):
+    nc = tc.nc
+    with ExitStack() as ctx:
+        keep = ctx.enter_context(tc.tile_pool(name="keep", bufs=1))
+        psum = ctx.enter_context(tc.psum_pool(name="psum", bufs=1))
+
+        def load_list(src, name):
+            t = keep.tile([P, src.shape[1]], U16, name=name)
+            nc.sync.dma_start(t[:], src)
+            return t
+
+        def load_words(src, name):
+            t = keep.tile([P, src.shape[2]], I32, name=name)
+            nc.sync.dma_start(t[:], src[0].rearrange("p c d -> p (c d)").bitcast(I32))
+            return t
+
+        def zeroed_plane(src, name):
+            t = keep.tile([P, src.shape[2]], U8, name=name)
+            nc.vector.memset(t[:].bitcast(I32), 0)
+            return t
+
+        def load_scales(t, src):
+            for r in range(4):
+                nc.sync.dma_start(t[r:P:32, :].bitcast(I32), src[0, r:16:4, :].bitcast(I32))
+
+        def gather_words(table, lst, a, b, name):
+            t = keep.tile([P, b - a], I32, name=name, align_bytes=64)
+            nc.vector.tensor_copy(t[:].bitcast(U32), table[:].bitcast(U32).indirect(lst[:, a // 16 : b // 16]))
+            return t
+
+        def gather_scales(table, lst, a, b, name):
+            t = keep.tile([P, b - a], U8, name=name, align_bytes=64)
+            nc.vector.tensor_copy(t[:], table[:].indirect(lst[:, a // 16 : b // 16]))
+            return t
+
+        xs_all = zeroed_plane(x_scales, "xs_all")
+        w1s_all = zeroed_plane(w1_scales, "w1s_all")
+        w2s_all = zeroed_plane(w2_scales, "w2s_all")
+
+        tok = load_list(offs, "tok")
+        xw_all = load_words(x_words, "xw_all")
+        load_scales(xs_all, x_scales)
+        col2 = load_list(offs3, "col2")
+        w2w_all = load_words(w2_words, "w2w_all")
+        col1 = load_list(offs2, "col1")
+        load_scales(w1s_all, w1_scales)
+        w1w_all = load_words(w1_words, "w1w_all")
+        load_scales(w2s_all, w2_scales)
+        g = keep.tile([P, S * B], F32, name="g")
+        nc.sync.dma_start(g[:], gate)
+
+        ident = keep.tile([P, P], F32, name="ident")
+        make_identity(nc, ident[:])
+
+        xw = [gather_words(xw_all, tok, 256 * j, 256 * j + 256, "xw%d" % j) for j in range(2)]
+        xs = [gather_scales(xs_all, tok, 256 * j, 256 * j + 256, "xs%d" % j) for j in range(2)]
+        w2w = gather_words(w2w_all, col2, 0, B * N, "w2w")
+        w1s = gather_scales(w1s_all, col1, 0, B * H, "w1s")
+
+        hT = [keep.tile([P, 2 * S * 4], BF16, name="hT%d" % j, align_bytes=64) for j in range(2)]
+        for m in range(B):
+            j, u = divmod(m, 2)
+            w1w = gather_words(w1w_all, col1, H * m, H * m + H, "w1w%d" % m)
+            pre = psum.tile([P, H], F32, name="pre", tag="pre", bufs=3)
+            nc.tensor.matmul_mx(
+                out=pre[:],
+                lhsT=xw[j][:, S * u : S * u + S].bitcast(FP8X4),
+                lhsT_scale=xs[j][:, S * u : S * u + S],
+                rhs=w1w[:].bitcast(FP8X4),
+                rhs_scale=w1s[:, H * m : H * m + H],
+                start=True,
+                stop=True,
+            )
+            hs = keep.tile([P, H], BF16, name="hs%d" % m)
+            nc.scalar.activation(
+                hs[:].rearrange("s (v p e) -> s v p e", v=2, e=2),
+                pre[:].rearrange("s (p v e) -> s v p e", v=2, e=2),
+                mybir.ActivationFunctionType.Silu,
+            )
+            turned = psum.tile([P, 2, S], F32, name="turned", tag="turned", bufs=3)
+            for v in range(2):
+                nc.tensor.transpose(turned[:, v, :], hs[:].bitcast(F32)[:, P * v : P * v + P], ident[:])
+            nc.scalar.copy(
+                hT[j][:].bitcast(F32)[:, 2 * S * u : 2 * S * u + 2 * S].rearrange("p (s v) -> p s v", v=2),
+                turned[:].rearrange("p v s -> p s v"),
+            )
+
+        res = [keep.tile([P, T], F32, name="res%d" % a) for a in range(2)]
+        ys = []
+        for j in range(2):
+            w2s = gather_scales(w2s_all, col2, 2 * N * j, 2 * N * j + 2 * N, "w2s%d" % j)
+            hq = keep.tile([P, 2 * S], I32, name="hq%d" % j, align_bytes=64)
+            hqs = keep.tile([P, 2 * S], U8, name="hqs%d" % j, align_bytes=64)
+            nc.vector.quantize_mx(out=hq[:].bitcast(FP8X4), scales=hqs[:], in_=hT[j][:])
+            acc = psum.tile([P, 2, 2 * S], F32, name="acc", tag="acc", bufs=2)
+            for a in range(2):
+                for u in range(2):
+                    c = N * (2 * j + u) + P * a
+                    nc.tensor.matmul_mx(
+                        out=acc[:, a, S * u : S * u + S],
+                        lhsT=w2w[:, c : c + P].bitcast(FP8X4),
+                        lhsT_scale=w2s[:, c - 2 * N * j : c - 2 * N * j + P],
+                        rhs=hq[:, S * u : S * u + S].bitcast(FP8X4),
+                        rhs_scale=hqs[:, S * u : S * u + S],
+                        start=True,
+                        stop=True,
+                    )
+            y = keep.tile([P, 2, 2 * S], F32, name="y%d" % j)
+            nc.scalar.copy(y[:], acc[:])
+            ys.append(y)
+        for j in range(2):
+            for a in range(2):
+                nc.vector.tensor_tensor(
+                    res[a][:].indirect(tok[:, 16 * j : 16 * j + 16]),
+                    ys[j][:, a, :],
+                    g[:, 2 * S * j : 2 * S * j + 2 * S],
+                    mybir.AluOpType.mult,
+                )
+        for a in range(2):
+            nc.sync.dma_start(out[P * a : P * a + P, :], res[a][:])

@@ -44,45 +44,44 @@ def tile_moe_dyn_silu_kernel(
             for r in range(4):
                 nc.sync.dma_start(t[r:P:32, :].bitcast(I32), src[0, r:16:4, :].bitcast(I32))
 
-        def gather_words(table, lst, a, b, name):
-            t = keep.tile([P, b - a], I32, name=name, align_bytes=64)
+        def gather_words(table, lst, a, b, name, tag=""):
+            t = keep.tile([P, b - a], I32, name=name, tag=tag or name, align_bytes=64)
             nc.vector.tensor_copy(t[:].bitcast(U32), table[:].bitcast(U32).indirect(lst[:, a // 16 : b // 16]))
             return t
 
-        def gather_scales(table, lst, a, b, name):
-            t = keep.tile([P, b - a], U8, name=name, align_bytes=64)
+        def gather_scales(table, lst, a, b, name, tag=""):
+            t = keep.tile([P, b - a], U8, name=name, tag=tag or name, align_bytes=64)
             nc.vector.tensor_copy(t[:], table[:].indirect(lst[:, a // 16 : b // 16]))
             return t
 
         xs_all = zeroed_plane(x_scales, "xs_all")
         w1s_all = zeroed_plane(w1_scales, "w1s_all")
         w2s_all = zeroed_plane(w2_scales, "w2s_all")
+        ident = keep.tile([P, P], F32, name="ident")
+        nc.vector.memset(ident[:], 0.0)
+        make_identity(nc, ident[:], nomemset=True)
 
         tok = load_list(offs, "tok")
         xw_all = load_words(x_words, "xw_all")
         load_scales(xs_all, x_scales)
+        load_scales(w1s_all, w1_scales)
+        col1 = load_list(offs2, "col1")
+        w1w_all = load_words(w1_words, "w1w_all")
         col2 = load_list(offs3, "col2")
         w2w_all = load_words(w2_words, "w2w_all")
-        col1 = load_list(offs2, "col1")
-        load_scales(w1s_all, w1_scales)
-        w1w_all = load_words(w1_words, "w1w_all")
         load_scales(w2s_all, w2_scales)
         g = keep.tile([P, S * B], F32, name="g")
         nc.sync.dma_start(g[:], gate)
 
-        ident = keep.tile([P, P], F32, name="ident")
-        make_identity(nc, ident[:])
-
         xw = [gather_words(xw_all, tok, 256 * j, 256 * j + 256, "xw%d" % j) for j in range(2)]
         xs = [gather_scales(xs_all, tok, 256 * j, 256 * j + 256, "xs%d" % j) for j in range(2)]
-        w2w = gather_words(w2w_all, col2, 0, B * N, "w2w")
         w1s = gather_scales(w1s_all, col1, 0, B * H, "w1s")
 
-        hT = [keep.tile([P, 2 * S * 4], BF16, name="hT%d" % j, align_bytes=64) for j in range(2)]
+        hT = []
         for m in range(B):
             j, u = divmod(m, 2)
             w1w = gather_words(w1w_all, col1, H * m, H * m + H, "w1w%d" % m)
-            pre = psum.tile([P, H], F32, name="pre", tag="pre", bufs=3)
+            pre = psum.tile([P, H], F32, name="pre", tag="pre", bufs=2)
             nc.tensor.matmul_mx(
                 out=pre[:],
                 lhsT=xw[j][:, S * u : S * u + S].bitcast(FP8X4),
@@ -92,48 +91,54 @@ def tile_moe_dyn_silu_kernel(
                 start=True,
                 stop=True,
             )
-            hs = keep.tile([P, H], BF16, name="hs%d" % m)
+            hs = keep.tile([P, H], BF16, name="hs%d" % m, tag="hs%d" % m, align_bytes=64)
             nc.scalar.activation(
                 hs[:].rearrange("s (v p e) -> s v p e", v=2, e=2),
                 pre[:].rearrange("s (p v e) -> s v p e", v=2, e=2),
                 mybir.ActivationFunctionType.Silu,
             )
-            turned = psum.tile([P, 2, S], F32, name="turned", tag="turned", bufs=3)
+            turned = psum.tile([P, 2, S], F32, name="turned", tag="turned", bufs=2)
             for v in range(2):
                 nc.tensor.transpose(turned[:, v, :], hs[:].bitcast(F32)[:, P * v : P * v + P], ident[:])
+            ht = keep.tile([P, 4 * S], BF16, name="hT%d" % m, tag="hT%d" % m, align_bytes=64)
             nc.scalar.copy(
-                hT[j][:].bitcast(F32)[:, 2 * S * u : 2 * S * u + 2 * S].rearrange("p (s v) -> p s v", v=2),
+                ht[:].bitcast(F32).rearrange("p (s v) -> p s v", v=2),
                 turned[:].rearrange("p v s -> p s v"),
             )
+            hT.append(ht)
 
         res = [keep.tile([P, T], F32, name="res%d" % a) for a in range(2)]
         ys = []
+        w2w = gather_words(w2w_all, col2, 0, B * N, "w2w")
         for j in range(2):
-            w2s = gather_scales(w2s_all, col2, 2 * N * j, 2 * N * j + 2 * N, "w2s%d" % j)
-            hq = keep.tile([P, 2 * S], I32, name="hq%d" % j, align_bytes=64)
-            hqs = keep.tile([P, 2 * S], U8, name="hqs%d" % j, align_bytes=64)
-            nc.vector.quantize_mx(out=hq[:].bitcast(FP8X4), scales=hqs[:], in_=hT[j][:])
-            acc = psum.tile([P, 2, 2 * S], F32, name="acc", tag="acc", bufs=2)
+            w2s = gather_scales(w2s_all, col2, 2 * N * j, 2 * N * j + 2 * N, "w2s%d" % j, tag="hT0" if j else "hs3")
+            hq, hqs = [], []
+            for u in range(2):
+                m = 2 * j + u
+                hq.append(keep.tile([P, S], I32, name="hq%d" % m, align_bytes=64))
+                hqs.append(keep.tile([P, S], U8, name="hqs%d" % m, align_bytes=64))
+                nc.vector.quantize_mx(out=hq[u][:].bitcast(FP8X4), scales=hqs[u][:], in_=hT[m][:])
             for a in range(2):
+                acc = psum.tile([P, 2 * S], F32, name="acc", tag="acc", bufs=4)
                 for u in range(2):
-                    c = N * (2 * j + u) + P * a
+                    c = N * u + P * a
                     nc.tensor.matmul_mx(
-                        out=acc[:, a, S * u : S * u + S],
-                        lhsT=w2w[:, c : c + P].bitcast(FP8X4),
-                        lhsT_scale=w2s[:, c - 2 * N * j : c - 2 * N * j + P],
-                        rhs=hq[:, S * u : S * u + S].bitcast(FP8X4),
-                        rhs_scale=hqs[:, S * u : S * u + S],
+                        out=acc[:, S * u : S * u + S],
+                        lhsT=w2w[:, 2 * N * j + c : 2 * N * j + c + P].bitcast(FP8X4),
+                        lhsT_scale=w2s[:, c : c + P],
+                        rhs=hq[u][:].bitcast(FP8X4),
+                        rhs_scale=hqs[u][:],
                         start=True,
                         stop=True,
                     )
-            y = keep.tile([P, 2, 2 * S], F32, name="y%d" % j)
-            nc.scalar.copy(y[:], acc[:])
-            ys.append(y)
+                y = keep.tile([P, 2 * S], F32, name="y%d%d" % (j, a))
+                nc.scalar.copy(y[:], acc[:])
+                ys.append(y)
         for j in range(2):
             for a in range(2):
                 nc.vector.tensor_tensor(
                     res[a][:].indirect(tok[:, 16 * j : 16 * j + 16]),
-                    ys[j][:, a, :],
+                    ys[2 * j + a][:],
                     g[:, 2 * S * j : 2 * S * j + 2 * S],
                     mybir.AluOpType.mult,
                 )

@@ -15,6 +15,7 @@ U8 = mybir.dt.uint8
 FP8X4 = mybir.dt.float8_e4m3fn_x4
 P = 128
 S = 128
+X_ROW, W1_ROW, W2_ROW = 0, 4, 8
 
 
 def tile_moe_dyn_silu_kernel(
@@ -40,9 +41,9 @@ def tile_moe_dyn_silu_kernel(
             nc.vector.memset(t[:].bitcast(I32), 0)
             return t
 
-        def load_scales(t, src):
-            for r in range(4):
-                nc.sync.dma_start(t[r:P:32, :].bitcast(I32), src[0, r:16:4, :].bitcast(I32))
+        def load_scales(queue, t, src, row, rs=range(4)):
+            for r in rs:
+                queue.dma_start(t[row + r : P : 32, :].bitcast(I32), src[0, r:16:4, :].bitcast(I32))
 
         def gather_words(table, lst, a, b, name, tag=""):
             t = keep.tile([P, b - a], I32, name=name, tag=tag or name, align_bytes=64)
@@ -54,8 +55,8 @@ def tile_moe_dyn_silu_kernel(
             nc.vector.tensor_copy(t[:], table[:].indirect(lst[:, a // 16 : b // 16]))
             return t
 
-        xs_all = zeroed_plane(x_scales, "xs_all")
         w1s_all = zeroed_plane(w1_scales, "w1s_all")
+        xs_all = zeroed_plane(x_scales, "xs_all")
         w2s_all = zeroed_plane(w2_scales, "w2s_all")
         ident = keep.tile([P, P], F32, name="ident")
         nc.vector.memset(ident[:], 0.0)
@@ -63,31 +64,31 @@ def tile_moe_dyn_silu_kernel(
 
         tok = load_list(offs, "tok")
         xw_all = load_words(x_words, "xw_all")
-        load_scales(xs_all, x_scales)
-        load_scales(w1s_all, w1_scales)
         col1 = load_list(offs2, "col1")
-        w1w_all = load_words(w1_words, "w1w_all")
+        load_scales(nc.sync, w1s_all, w1_scales, W1_ROW)
         col2 = load_list(offs3, "col2")
+        w1w_all = load_words(w1_words, "w1w_all")
+        load_scales(nc.scalar, xs_all, x_scales, X_ROW)
         w2w_all = load_words(w2_words, "w2w_all")
-        load_scales(w2s_all, w2_scales)
+        load_scales(nc.scalar, w2s_all, w2_scales, W2_ROW)
         g = keep.tile([P, S * B], F32, name="g")
         nc.sync.dma_start(g[:], gate)
 
         xw = [gather_words(xw_all, tok, 256 * j, 256 * j + 256, "xw%d" % j) for j in range(2)]
-        xs = [gather_scales(xs_all, tok, 256 * j, 256 * j + 256, "xs%d" % j) for j in range(2)]
         w1s = gather_scales(w1s_all, col1, 0, B * H, "w1s")
+        xs = [gather_scales(xs_all, tok, 256 * j, 256 * j + 256, "xs%d" % j) for j in range(2)]
 
         hT = []
         for m in range(B):
             j, u = divmod(m, 2)
             w1w = gather_words(w1w_all, col1, H * m, H * m + H, "w1w%d" % m)
-            pre = psum.tile([P, H], F32, name="pre", tag="pre", bufs=2)
+            pre = psum.tile([P, H], F32, name="pre", tag="pre", bufs=3)
             nc.tensor.matmul_mx(
                 out=pre[:],
                 lhsT=xw[j][:, S * u : S * u + S].bitcast(FP8X4),
-                lhsT_scale=xs[j][:, S * u : S * u + S],
+                lhsT_scale=xs[j][X_ROW:, S * u : S * u + S],
                 rhs=w1w[:].bitcast(FP8X4),
-                rhs_scale=w1s[:, H * m : H * m + H],
+                rhs_scale=w1s[W1_ROW:, H * m : H * m + H],
                 start=True,
                 stop=True,
             )
@@ -107,39 +108,36 @@ def tile_moe_dyn_silu_kernel(
             )
             hT.append(ht)
 
-        res = [keep.tile([P, T], F32, name="res%d" % a) for a in range(2)]
-        ys = []
+        w2s = gather_scales(w2s_all, col2, 0, B * N, "w2s")
         w2w = gather_words(w2w_all, col2, 0, B * N, "w2w")
-        for j in range(2):
-            w2s = gather_scales(w2s_all, col2, 2 * N * j, 2 * N * j + 2 * N, "w2s%d" % j, tag="hT0" if j else "hs3")
-            hq, hqs = [], []
-            for u in range(2):
-                m = 2 * j + u
-                hq.append(keep.tile([P, S], I32, name="hq%d" % m, align_bytes=64))
-                hqs.append(keep.tile([P, S], U8, name="hqs%d" % m, align_bytes=64))
-                nc.vector.quantize_mx(out=hq[u][:].bitcast(FP8X4), scales=hqs[u][:], in_=hT[m][:])
-            for a in range(2):
-                acc = psum.tile([P, 2 * S], F32, name="acc", tag="acc", bufs=4)
-                for u in range(2):
-                    c = N * u + P * a
+
+        res = [keep.tile([P, T], F32, name="res%d" % a) for a in range(2)]
+        for first, last in ((0, 1), (1, 2), (2, 4)):
+            width = S * (last - first)
+            y = keep.tile([P, 2, width], F32, name="y%d" % first)
+            for m in range(first, last):
+                hq = keep.tile([P, S], I32, name="hq%d" % m, align_bytes=64)
+                hqs = keep.tile([P, S], U8, name="hqs%d" % m, align_bytes=64)
+                nc.vector.quantize_mx(out=hq[:].bitcast(FP8X4), scales=hqs[:], in_=hT[m][:])
+                acc = psum.tile([P, 2, S], F32, name="acc", tag="acc", bufs=3)
+                for a in range(2):
+                    c = N * m + P * a
                     nc.tensor.matmul_mx(
-                        out=acc[:, S * u : S * u + S],
-                        lhsT=w2w[:, 2 * N * j + c : 2 * N * j + c + P].bitcast(FP8X4),
-                        lhsT_scale=w2s[:, c : c + P],
-                        rhs=hq[u][:].bitcast(FP8X4),
-                        rhs_scale=hqs[u][:],
+                        out=acc[:, a, :],
+                        lhsT=w2w[:, c : c + P].bitcast(FP8X4),
+                        lhsT_scale=w2s[W2_ROW:, c : c + P],
+                        rhs=hq[:].bitcast(FP8X4),
+                        rhs_scale=hqs[:],
                         start=True,
                         stop=True,
                     )
-                y = keep.tile([P, 2 * S], F32, name="y%d%d" % (j, a))
-                nc.scalar.copy(y[:], acc[:])
-                ys.append(y)
-        for j in range(2):
+                u = m - first
+                nc.scalar.copy(y[:, :, S * u : S * u + S], acc[:])
             for a in range(2):
                 nc.vector.tensor_tensor(
-                    res[a][:].indirect(tok[:, 16 * j : 16 * j + 16]),
-                    ys[2 * j + a][:],
-                    g[:, 2 * S * j : 2 * S * j + 2 * S],
+                    res[a][:].indirect(tok[:, 8 * first : 8 * last]),
+                    y[:, a, :],
+                    g[:, S * first : S * last],
                     mybir.AluOpType.mult,
                 )
         for a in range(2):

@@ -1,7 +1,6 @@
 from contextlib import ExitStack
 
 import concourse.mybir as mybir
-from concourse.masks import make_identity
 
 K, T, E, B, H, N = 512, 512, 8, 4, 512, 256
 FLOPS = 2 * 128 * B * (K * H + H * N)
@@ -16,6 +15,7 @@ FP8X4 = mybir.dt.float8_e4m3fn_x4
 P = 128
 S = 128
 X_ROW, W1_ROW, W2_ROW = 0, 4, 8
+STAGE = P - 16
 
 
 def tile_moe_dyn_silu_kernel(
@@ -37,7 +37,7 @@ def tile_moe_dyn_silu_kernel(
             return t
 
         def zeroed_plane(src, name):
-            t = keep.tile([P, src.shape[2]], U8, name=name)
+            t = keep.tile([P, src.shape[2]], U8, name=name, tag=name, align_bytes=64)
             nc.vector.memset(t[:].bitcast(I32), 0)
             return t
 
@@ -55,60 +55,67 @@ def tile_moe_dyn_silu_kernel(
             nc.vector.tensor_copy(t[:], table[:].indirect(lst[:, a // 16 : b // 16]))
             return t
 
+        xs_all = keep.tile([P, T], U8, name="xs_all", tag="xs_all")
+        nc.gpsimd.memset(xs_all[:].bitcast(I32), 0)
         w1s_all = zeroed_plane(w1_scales, "w1s_all")
-        xs_all = zeroed_plane(x_scales, "xs_all")
-        w2s_all = zeroed_plane(w2_scales, "w2s_all")
-        ident = keep.tile([P, P], F32, name="ident")
-        nc.vector.memset(ident[:], 0.0)
-        make_identity(nc, ident[:], nomemset=True)
+        w2s_all = keep.tile([P, E * N], U8, name="w2s_all")
+        nc.vector.memset(w2s_all[:STAGE, :].bitcast(I32), 0)
+        w2s = keep.tile([P, B * N], U8, name="w2s", align_bytes=64)
+        nc.vector.memset(w2s[:].bitcast(I32), 0)
 
         tok = load_list(offs, "tok")
-        xw_all = load_words(x_words, "xw_all")
+        xw_all = keep.tile([P, T], I32, name="xw_all", tag="xw_all")
+        nc.sync.dma_start(xw_all[:], x_words[0].rearrange("p c d -> p (c d)").bitcast(I32))
         col1 = load_list(offs2, "col1")
-        load_scales(nc.sync, w1s_all, w1_scales, W1_ROW)
         col2 = load_list(offs3, "col2")
+        nc.sync.dma_start(w2s_all[STAGE:, :].bitcast(I32), w2_scales[0].bitcast(I32))
+        load_scales(nc.sync, w1s_all, w1_scales, W1_ROW)
         w1w_all = load_words(w1_words, "w1w_all")
-        load_scales(nc.scalar, xs_all, x_scales, X_ROW)
         w2w_all = load_words(w2_words, "w2w_all")
-        load_scales(nc.scalar, w2s_all, w2_scales, W2_ROW)
-        g = keep.tile([P, S * B], F32, name="g")
-        nc.sync.dma_start(g[:], gate)
+        load_scales(nc.scalar, xs_all, x_scales, X_ROW)
 
         xw = [gather_words(xw_all, tok, 256 * j, 256 * j + 256, "xw%d" % j) for j in range(2)]
+        w2s_staged = gather_scales(w2s_all, col2, 0, B * N, "w2s_staged")
+        for r in range(4):
+            nc.sync.dma_start(w2s[W2_ROW + r : P : 32, :].bitcast(I32), w2s_staged[STAGE + r : P : 4, :].bitcast(I32))
+        xs = [gather_scales(xs_all, tok, 0, 256, "xs0")]
         w1s = gather_scales(w1s_all, col1, 0, B * H, "w1s")
-        xs = [gather_scales(xs_all, tok, 256 * j, 256 * j + 256, "xs%d" % j) for j in range(2)]
+        xs.append(gather_scales(xs_all, tok, 256, 512, "xs1"))
+        g = keep.tile([P, S * B], F32, name="g", tag="xs_all")
+        nc.sync.dma_start(g[:], gate)
 
         hT = []
         for m in range(B):
             j, u = divmod(m, 2)
-            w1w = gather_words(w1w_all, col1, H * m, H * m + H, "w1w%d" % m)
-            pre = psum.tile([P, H], F32, name="pre", tag="pre", bufs=3)
-            nc.tensor.matmul_mx(
-                out=pre[:],
-                lhsT=xw[j][:, S * u : S * u + S].bitcast(FP8X4),
-                lhsT_scale=xs[j][X_ROW:, S * u : S * u + S],
-                rhs=w1w[:].bitcast(FP8X4),
-                rhs_scale=w1s[W1_ROW:, H * m : H * m + H],
-                start=True,
-                stop=True,
+            w1p = keep.tile([P, H], U8, name="w1p%d" % m, tag="w1p", bufs=2, align_bytes=64)
+            nc.vector.tensor_copy(
+                w1p[:].rearrange("p (t c) -> p t c", t=4),
+                w1s[:, H * m : H * m + H].rearrange("p (c t) -> p t c", t=4),
             )
-            hs = keep.tile([P, H], BF16, name="hs%d" % m, tag="hs%d" % m, align_bytes=64)
-            nc.scalar.activation(
-                hs[:].rearrange("s (v p e) -> s v p e", v=2, e=2),
-                pre[:].rearrange("s (p v e) -> s v p e", v=2, e=2),
-                mybir.ActivationFunctionType.Silu,
+            w1w = keep.tile([P, H], I32, name="w1w%d" % m, tag="w1w%d" % m if m else "w1s_all", align_bytes=64)
+            nc.vector.tensor_copy(
+                w1w[:].bitcast(U32).rearrange("p (t c) -> p c t", t=4),
+                w1w_all[:].bitcast(U32).indirect(col1[:, H * m // 16 : (H * m + H) // 16]),
             )
-            turned = psum.tile([P, 2, S], F32, name="turned", tag="turned", bufs=2)
-            for v in range(2):
-                nc.tensor.transpose(turned[:, v, :], hs[:].bitcast(F32)[:, P * v : P * v + P], ident[:])
+            pre = psum.tile([P, 4, S], F32, name="pre", tag="pre", bufs=4)
+            for t in range(4):
+                nc.tensor.matmul_mx(
+                    out=pre[:, t, :],
+                    lhsT=w1w[:, P * t : P * t + P].bitcast(FP8X4),
+                    lhsT_scale=w1p[W1_ROW:, P * t : P * t + P],
+                    rhs=xw[j][:, S * u : S * u + S].bitcast(FP8X4),
+                    rhs_scale=xs[j][X_ROW:, S * u : S * u + S],
+                    start=True,
+                    stop=True,
+                )
             ht = keep.tile([P, 4 * S], BF16, name="hT%d" % m, tag="hT%d" % m, align_bytes=64)
-            nc.scalar.copy(
-                ht[:].bitcast(F32).rearrange("p (s v) -> p s v", v=2),
-                turned[:].rearrange("p v s -> p s v"),
+            nc.scalar.activation(
+                ht[:].rearrange("p (s t) -> p s t", t=4),
+                pre[:].rearrange("p t s -> p s t"),
+                mybir.ActivationFunctionType.Silu,
             )
             hT.append(ht)
 
-        w2s = gather_scales(w2s_all, col2, 0, B * N, "w2s")
         w2w = gather_words(w2w_all, col2, 0, B * N, "w2w")
 
         res = [keep.tile([P, T], F32, name="res%d" % a) for a in range(2)]

@@ -1,6 +1,7 @@
 from contextlib import ExitStack
 
 import concourse.mybir as mybir
+from concourse.masks import make_identity
 
 K, T, E, B, H, N = 512, 512, 8, 4, 512, 256
 FLOPS = 2 * 128 * B * (K * H + H * N)
@@ -15,7 +16,6 @@ FP8X4 = mybir.dt.float8_e4m3fn_x4
 P = 128
 S = 128
 X_ROW, W1_ROW, W2_ROW = 0, 4, 8
-STAGE = P - 16
 
 
 def tile_moe_dyn_silu_kernel(
@@ -26,126 +26,180 @@ def tile_moe_dyn_silu_kernel(
         keep = ctx.enter_context(tc.tile_pool(name="keep", bufs=1))
         psum = ctx.enter_context(tc.psum_pool(name="psum", bufs=1))
 
+        def tile(width, dtype, name, over=""):
+            return keep.tile([P, width], dtype, name=name, tag=over or name, align_bytes=64)
+
         def load_list(src, name):
             t = keep.tile([P, src.shape[1]], U16, name=name)
             nc.sync.dma_start(t[:], src)
             return t
 
         def load_words(src, name):
-            t = keep.tile([P, src.shape[2]], I32, name=name)
+            t = tile(src.shape[2], I32, name)
             nc.sync.dma_start(t[:], src[0].rearrange("p c d -> p (c d)").bitcast(I32))
             return t
 
-        def zeroed_plane(src, name):
-            t = keep.tile([P, src.shape[2]], U8, name=name, tag=name, align_bytes=64)
-            nc.vector.memset(t[:].bitcast(I32), 0)
-            return t
-
-        def load_scales(queue, t, src, row, rs=range(4)):
-            for r in rs:
+        def load_scales(queue, t, src, row):
+            for r in range(4):
                 queue.dma_start(t[row + r : P : 32, :].bitcast(I32), src[0, r:16:4, :].bitcast(I32))
 
-        def gather_words(table, lst, a, b, name, tag=""):
-            t = keep.tile([P, b - a], I32, name=name, tag=tag or name, align_bytes=64)
+        def gather_words(table, lst, a, b, name, over=""):
+            t = tile(b - a, I32, name, over)
             nc.vector.tensor_copy(t[:].bitcast(U32), table[:].bitcast(U32).indirect(lst[:, a // 16 : b // 16]))
             return t
 
-        def gather_scales(table, lst, a, b, name, tag=""):
-            t = keep.tile([P, b - a], U8, name=name, tag=tag or name, align_bytes=64)
+        def gather_scales(table, lst, a, b, name, over=""):
+            t = tile(b - a, U8, name, over)
             nc.vector.tensor_copy(t[:], table[:].indirect(lst[:, a // 16 : b // 16]))
             return t
 
-        xs_all = keep.tile([P, T], U8, name="xs_all", tag="xs_all")
+        xs_all = tile(T, U8, "xs_all")
         nc.gpsimd.memset(xs_all[:].bitcast(I32), 0)
-        w1s_all = zeroed_plane(w1_scales, "w1s_all")
-        w2s_all = keep.tile([P, E * N], U8, name="w2s_all")
-        nc.vector.memset(w2s_all[:STAGE, :].bitcast(I32), 0)
-        w2s = keep.tile([P, B * N], U8, name="w2s", align_bytes=64)
-        nc.vector.memset(w2s[:].bitcast(I32), 0)
+        w1s_all = tile(E * H, U8, "w1s_all")
+        nc.vector.memset(w1s_all[:].bitcast(I32), 0)
+        w2s_all = tile(E * N, U8, "w2s_all")
+        nc.vector.memset(w2s_all[:].bitcast(I32), 0)
+        ident = keep.tile([P, P], F32, name="ident")
+        nc.vector.memset(ident[:], 0.0)
+        make_identity(nc, ident[:], nomemset=True)
 
         tok = load_list(offs, "tok")
-        xw_all = keep.tile([P, T], I32, name="xw_all", tag="xw_all")
-        nc.sync.dma_start(xw_all[:], x_words[0].rearrange("p c d -> p (c d)").bitcast(I32))
+        xw_all = load_words(x_words, "xw_all")
         col1 = load_list(offs2, "col1")
-        col2 = load_list(offs3, "col2")
-        nc.sync.dma_start(w2s_all[STAGE:, :].bitcast(I32), w2_scales[0].bitcast(I32))
+        w1w_all = tile(E * H, I32, "w1w_all")
+        w1_view = w1_words[0].rearrange("p c d -> p (c d)").bitcast(I32)
         load_scales(nc.sync, w1s_all, w1_scales, W1_ROW)
-        w1w_all = load_words(w1_words, "w1w_all")
+        nc.sync.dma_start(w1w_all[:, :2048], w1_view[:, :2048])
+        load_scales(nc.sync, xs_all, x_scales, X_ROW)
+        nc.sync.dma_start(w1w_all[:, 2048:], w1_view[:, 2048:])
+        col2 = load_list(offs3, "col2")
+        load_scales(nc.sync, w2s_all, w2_scales, W2_ROW)
         w2w_all = load_words(w2_words, "w2w_all")
-        load_scales(nc.scalar, xs_all, x_scales, X_ROW)
-
-        xw = [gather_words(xw_all, tok, 256 * j, 256 * j + 256, "xw%d" % j) for j in range(2)]
-        w2s_staged = gather_scales(w2s_all, col2, 0, B * N, "w2s_staged")
-        for r in range(4):
-            nc.sync.dma_start(w2s[W2_ROW + r : P : 32, :].bitcast(I32), w2s_staged[STAGE + r : P : 4, :].bitcast(I32))
-        xs = [gather_scales(xs_all, tok, 0, 256, "xs0")]
-        w1s = gather_scales(w1s_all, col1, 0, B * H, "w1s")
-        xs.append(gather_scales(xs_all, tok, 256, 512, "xs1"))
-        g = keep.tile([P, S * B], F32, name="g", tag="xs_all")
+        g = tile(S * B, F32, "g")
         nc.sync.dma_start(g[:], gate)
 
-        hT = []
-        for m in range(B):
-            j, u = divmod(m, 2)
-            w1p = keep.tile([P, H], U8, name="w1p%d" % m, tag="w1p", bufs=2, align_bytes=64)
+        w1p, w1w, hT, hq, hqs, y = {}, {}, {}, {}, {}, {}
+        res = [keep.tile([P, T], F32, name="res%d" % a) for a in range(2)]
+
+        def permute_scales(m, over=""):
+            w1p[m] = tile(H, U8, "w1p%d" % m, over)
             nc.vector.tensor_copy(
-                w1p[:].rearrange("p (t c) -> p t c", t=4),
+                w1p[m][:].rearrange("p (t c) -> p t c", t=4),
                 w1s[:, H * m : H * m + H].rearrange("p (c t) -> p t c", t=4),
             )
-            w1w = keep.tile([P, H], I32, name="w1w%d" % m, tag="w1w%d" % m if m else "w1s_all", align_bytes=64)
+
+        def gather_w1(m, over=""):
+            w1w[m] = tile(H, I32, "w1w%d" % m, over)
             nc.vector.tensor_copy(
-                w1w[:].bitcast(U32).rearrange("p (t c) -> p c t", t=4),
+                w1w[m][:].bitcast(U32).rearrange("p (t c) -> p c t", t=4),
                 w1w_all[:].bitcast(U32).indirect(col1[:, H * m // 16 : (H * m + H) // 16]),
             )
-            pre = psum.tile([P, 4, S], F32, name="pre", tag="pre", bufs=4)
+
+        def first_layer(m):
+            j, u = divmod(m, 2)
+            pre = psum.tile([P, 4, S], F32, name="pre", tag="pre", bufs=3)
             for t in range(4):
                 nc.tensor.matmul_mx(
                     out=pre[:, t, :],
-                    lhsT=w1w[:, P * t : P * t + P].bitcast(FP8X4),
-                    lhsT_scale=w1p[W1_ROW:, P * t : P * t + P],
+                    lhsT=w1w[m][:, P * t : P * t + P].bitcast(FP8X4),
+                    lhsT_scale=w1p[m][W1_ROW:, P * t : P * t + P],
                     rhs=xw[j][:, S * u : S * u + S].bitcast(FP8X4),
                     rhs_scale=xs[j][X_ROW:, S * u : S * u + S],
                     start=True,
                     stop=True,
                 )
-            ht = keep.tile([P, 4 * S], BF16, name="hT%d" % m, tag="hT%d" % m, align_bytes=64)
+            hT[m] = tile(4 * S, BF16, "hT%d" % m)
             nc.scalar.activation(
-                ht[:].rearrange("p (s t) -> p s t", t=4),
+                hT[m][:].rearrange("p (s t) -> p s t", t=4),
                 pre[:].rearrange("p t s -> p s t"),
                 mybir.ActivationFunctionType.Silu,
             )
-            hT.append(ht)
 
-        w2w = gather_words(w2w_all, col2, 0, B * N, "w2w")
+        def first_layer_turned(m, over=""):
+            j, u = divmod(m, 2)
+            w1w[m] = gather_words(w1w_all, col1, H * m, H * m + H, "w1w%d" % m, over)
+            pre = psum.tile([P, H], F32, name="pre", tag="pre", bufs=3)
+            nc.tensor.matmul_mx(
+                out=pre[:],
+                lhsT=xw[j][:, S * u : S * u + S].bitcast(FP8X4),
+                lhsT_scale=xs[j][X_ROW:, S * u : S * u + S],
+                rhs=w1w[m][:].bitcast(FP8X4),
+                rhs_scale=w1s[W1_ROW:, H * m : H * m + H],
+                start=True,
+                stop=True,
+            )
+            hs = tile(H, BF16, "hs%d" % m)
+            nc.scalar.activation(
+                hs[:].rearrange("s (v p e) -> s v p e", v=2, e=2),
+                pre[:].rearrange("s (p v e) -> s v p e", v=2, e=2),
+                mybir.ActivationFunctionType.Silu,
+            )
+            turned = psum.tile([P, 2, S], F32, name="turned", tag="turned", bufs=2)
+            for v in range(2):
+                nc.tensor.transpose(turned[:, v, :], hs[:].bitcast(F32)[:, P * v : P * v + P], ident[:])
+            hT[m] = tile(4 * S, BF16, "hT%d" % m)
+            nc.scalar.copy(
+                hT[m][:].bitcast(F32).rearrange("p (s v) -> p s v", v=2),
+                turned[:].rearrange("p v s -> p s v"),
+            )
 
-        res = [keep.tile([P, T], F32, name="res%d" % a) for a in range(2)]
-        for first, last in ((0, 1), (1, 2), (2, 4)):
-            width = S * (last - first)
-            y = keep.tile([P, 2, width], F32, name="y%d" % first)
-            for m in range(first, last):
-                hq = keep.tile([P, S], I32, name="hq%d" % m, align_bytes=64)
-                hqs = keep.tile([P, S], U8, name="hqs%d" % m, align_bytes=64)
-                nc.vector.quantize_mx(out=hq[:].bitcast(FP8X4), scales=hqs[:], in_=hT[m][:])
-                acc = psum.tile([P, 2, S], F32, name="acc", tag="acc", bufs=3)
+        def second_layer(m, over="", parts=1):
+            j, u = divmod(m, 2)
+            hq[m] = tile(S, I32, "hq%d" % m, over)
+            hqs[m] = tile(S, U8, "hqs%d" % m)
+            nc.vector.quantize_mx(out=hq[m][:].bitcast(FP8X4), scales=hqs[m][:], in_=hT[m][:])
+            acc = psum.tile([P, 2, S], F32, name="acc", tag="acc", bufs=3)
+            for a in range(2):
+                c = N * u + P * a
+                nc.tensor.matmul_mx(
+                    out=acc[:, a, :],
+                    lhsT=w2w[j][:, c : c + P].bitcast(FP8X4),
+                    lhsT_scale=w2s[j][W2_ROW:, c : c + P],
+                    rhs=hq[m][:].bitcast(FP8X4),
+                    rhs_scale=hqs[m][:],
+                    start=True,
+                    stop=True,
+                )
+            if parts == 1:
+                both = tile(2 * S, F32, "y%d" % m)
+                nc.scalar.copy(both[:], acc[:].rearrange("p a s -> p (a s)"))
+                y[m] = [both[:, S * a : S * a + S] for a in range(2)]
+            else:
+                halves = [tile(S, F32, "y%d_%d" % (m, a)) for a in range(2)]
                 for a in range(2):
-                    c = N * m + P * a
-                    nc.tensor.matmul_mx(
-                        out=acc[:, a, :],
-                        lhsT=w2w[:, c : c + P].bitcast(FP8X4),
-                        lhsT_scale=w2s[W2_ROW:, c : c + P],
-                        rhs=hq[:].bitcast(FP8X4),
-                        rhs_scale=hqs[:],
-                        start=True,
-                        stop=True,
-                    )
-                u = m - first
-                nc.scalar.copy(y[:, :, S * u : S * u + S], acc[:])
+                    nc.scalar.copy(halves[a][:], acc[:, a, :])
+                y[m] = [half[:] for half in halves]
+
+        def scatter(m):
             for a in range(2):
                 nc.vector.tensor_tensor(
-                    res[a][:].indirect(tok[:, 8 * first : 8 * last]),
-                    y[:, a, :],
-                    g[:, S * first : S * last],
+                    res[a][:].indirect(tok[:, 8 * m : 8 * m + 8]),
+                    y[m][a],
+                    g[:, S * m : S * m + S],
                     mybir.AluOpType.mult,
                 )
+
+        xw = [gather_words(xw_all, tok, 256 * j, 256 * j + 256, "xw%d" % j) for j in range(2)]
+        w1s = gather_scales(w1s_all, col1, 0, B * H, "w1s")
+        permute_scales(0)
+        permute_scales(1)
+        xs = [gather_scales(xs_all, tok, 256 * j, 256 * j + 256, "xs%d" % j) for j in range(2)]
+        gather_w1(0)
+        first_layer(0)
+        gather_w1(1)
+        first_layer(1)
+        first_layer_turned(2)
+        first_layer_turned(3)
+        w2s = [gather_scales(w2s_all, col2, 0, 2 * N, "w2s0")]
+        w2w = [gather_words(w2w_all, col2, 2 * N * j, 2 * N * j + 2 * N, "w2w%d" % j) for j in range(2)]
+        second_layer(0, parts=2)
+        second_layer(1, over="hq0")
+        w2s.append(gather_scales(w2s_all, col2, 2 * N, 4 * N, "w2s1", over="hqs0"))
+        scatter(0)
+        second_layer(2, over="hT1")
+        second_layer(3, over="y0_0")
+        scatter(1)
+        scatter(2)
+        scatter(3)
         for a in range(2):
             nc.sync.dma_start(out[P * a : P * a + P, :], res[a][:])

@@ -13,8 +13,13 @@ U32 = mybir.dt.uint32
 U16 = mybir.dt.uint16
 U8 = mybir.dt.uint8
 FP8X4 = mybir.dt.float8_e4m3fn_x4
+
 P = 128
 S = 128
+PACK = 4
+LIST = 16
+PAIR = 2 * S
+HALVES = N // P
 X_ROW, W1_ROW, W2_ROW = 0, 4, 8
 
 
@@ -29,6 +34,9 @@ def tile_moe_dyn_silu_kernel(
         def tile(width, dtype, name, over=""):
             return keep.tile([P, width], dtype, name=name, tag=over or name, align_bytes=64)
 
+        def words_of(src):
+            return src[0].rearrange("p c d -> p (c d)").bitcast(I32)
+
         def load_list(src, name):
             t = keep.tile([P, src.shape[1]], U16, name=name)
             nc.sync.dma_start(t[:], src)
@@ -36,21 +44,24 @@ def tile_moe_dyn_silu_kernel(
 
         def load_words(src, name):
             t = tile(src.shape[2], I32, name)
-            nc.sync.dma_start(t[:], src[0].rearrange("p c d -> p (c d)").bitcast(I32))
+            nc.sync.dma_start(t[:], words_of(src))
             return t
 
-        def load_scales(queue, t, src, row):
-            for r in range(4):
-                queue.dma_start(t[row + r : P : 32, :].bitcast(I32), src[0, r:16:4, :].bitcast(I32))
+        def load_scales(t, src, row):
+            for q in range(4):
+                nc.sync.dma_start(t[row + q : P : 32, :].bitcast(I32), src[0, q:16:4, :].bitcast(I32))
 
-        def gather_words(table, lst, a, b, name, over=""):
-            t = tile(b - a, I32, name, over)
-            nc.vector.tensor_copy(t[:].bitcast(U32), table[:].bitcast(U32).indirect(lst[:, a // 16 : b // 16]))
+        def entries(lst, a, b):
+            return lst[:, a // LIST : b // LIST]
+
+        def gather_words(table, lst, a, b, name):
+            t = tile(b - a, I32, name)
+            nc.vector.tensor_copy(t[:].bitcast(U32), table[:].bitcast(U32).indirect(entries(lst, a, b)))
             return t
 
         def gather_scales(table, lst, a, b, name, over=""):
             t = tile(b - a, U8, name, over)
-            nc.vector.tensor_copy(t[:], table[:].indirect(lst[:, a // 16 : b // 16]))
+            nc.vector.tensor_copy(t[:], table[:].indirect(entries(lst, a, b)))
             return t
 
         xs_all = tile(T, U8, "xs_all")
@@ -67,139 +78,141 @@ def tile_moe_dyn_silu_kernel(
         xw_all = load_words(x_words, "xw_all")
         col1 = load_list(offs2, "col1")
         w1w_all = tile(E * H, I32, "w1w_all")
-        w1_view = w1_words[0].rearrange("p c d -> p (c d)").bitcast(I32)
-        load_scales(nc.sync, w1s_all, w1_scales, W1_ROW)
-        nc.sync.dma_start(w1w_all[:, :2048], w1_view[:, :2048])
-        load_scales(nc.sync, xs_all, x_scales, X_ROW)
-        nc.sync.dma_start(w1w_all[:, 2048:], w1_view[:, 2048:])
+        half = E * H // 2
+        load_scales(w1s_all, w1_scales, W1_ROW)
+        nc.sync.dma_start(w1w_all[:, :half], words_of(w1_words)[:, :half])
+        load_scales(xs_all, x_scales, X_ROW)
+        nc.sync.dma_start(w1w_all[:, half:], words_of(w1_words)[:, half:])
         col2 = load_list(offs3, "col2")
-        load_scales(nc.sync, w2s_all, w2_scales, W2_ROW)
+        load_scales(w2s_all, w2_scales, W2_ROW)
         w2w_all = load_words(w2_words, "w2w_all")
         g = tile(S * B, F32, "g")
         nc.sync.dma_start(g[:], gate)
 
-        w1p, w1w, hT, hq, hqs, y = {}, {}, {}, {}, {}, {}
-        res = [keep.tile([P, T], F32, name="res%d" % a) for a in range(2)]
+        w1p, hs, hT, y = {}, {}, {}, {}
+        res = [keep.tile([P, T], F32, name="res%d" % a) for a in range(HALVES)]
 
-        def permute_scales(m, over=""):
-            w1p[m] = tile(H, U8, "w1p%d" % m, over)
-            nc.vector.tensor_copy(
-                w1p[m][:].rearrange("p (t c) -> p t c", t=4),
-                w1s[:, H * m : H * m + H].rearrange("p (c t) -> p t c", t=4),
-            )
-
-        def gather_w1(m, over=""):
-            w1w[m] = tile(H, I32, "w1w%d" % m, over)
-            nc.vector.tensor_copy(
-                w1w[m][:].bitcast(U32).rearrange("p (t c) -> p c t", t=4),
-                w1w_all[:].bitcast(U32).indirect(col1[:, H * m // 16 : (H * m + H) // 16]),
-            )
-
-        def first_layer(m):
+        def slots(m):
             j, u = divmod(m, 2)
-            pre = psum.tile([P, 4, S], F32, name="pre", tag="pre", bufs=3)
-            for t in range(4):
+            cols = slice(S * u, S * u + S)
+            return xw[j][:, cols].bitcast(FP8X4), xs[j][X_ROW:, cols]
+
+        def permute_scales(m):
+            w1p[m] = tile(H, U8, "w1p%d" % m)
+            nc.vector.tensor_copy(
+                w1p[m][:].rearrange("p (t c) -> p t c", t=PACK),
+                w1s[:, H * m : H * m + H].rearrange("p (c t) -> p t c", t=PACK),
+            )
+
+        def first_layer_direct(m):
+            w1w = tile(H, I32, "w1w%d" % m)
+            nc.vector.tensor_copy(
+                w1w[:].bitcast(U32).rearrange("p (t c) -> p c t", t=PACK),
+                w1w_all[:].bitcast(U32).indirect(entries(col1, H * m, H * m + H)),
+            )
+            codes, scales = slots(m)
+            pre = psum.tile([P, PACK, S], F32, name="pre", tag="pre", bufs=B)
+            for t in range(PACK):
                 nc.tensor.matmul_mx(
                     out=pre[:, t, :],
-                    lhsT=w1w[m][:, P * t : P * t + P].bitcast(FP8X4),
+                    lhsT=w1w[:, P * t : P * t + P].bitcast(FP8X4),
                     lhsT_scale=w1p[m][W1_ROW:, P * t : P * t + P],
-                    rhs=xw[j][:, S * u : S * u + S].bitcast(FP8X4),
-                    rhs_scale=xs[j][X_ROW:, S * u : S * u + S],
+                    rhs=codes,
+                    rhs_scale=scales,
                     start=True,
                     stop=True,
                 )
-            hT[m] = tile(4 * S, BF16, "hT%d" % m)
+            hT[m] = tile(PACK * S, BF16, "hT%d" % m)
             nc.scalar.activation(
-                hT[m][:].rearrange("p (s t) -> p s t", t=4),
+                hT[m][:].rearrange("p (s t) -> p s t", t=PACK),
                 pre[:].rearrange("p t s -> p s t"),
                 mybir.ActivationFunctionType.Silu,
             )
 
-        def first_layer_turned(m, over=""):
-            j, u = divmod(m, 2)
-            w1w[m] = gather_words(w1w_all, col1, H * m, H * m + H, "w1w%d" % m, over)
-            pre = psum.tile([P, H], F32, name="pre", tag="pre", bufs=3)
+        def first_layer_turned(m):
+            w1w = gather_words(w1w_all, col1, H * m, H * m + H, "w1w%d" % m)
+            codes, scales = slots(m)
+            pre = psum.tile([P, H], F32, name="pre", tag="pre", bufs=B)
             nc.tensor.matmul_mx(
                 out=pre[:],
-                lhsT=xw[j][:, S * u : S * u + S].bitcast(FP8X4),
-                lhsT_scale=xs[j][X_ROW:, S * u : S * u + S],
-                rhs=w1w[m][:].bitcast(FP8X4),
+                lhsT=codes,
+                lhsT_scale=scales,
+                rhs=w1w[:].bitcast(FP8X4),
                 rhs_scale=w1s[W1_ROW:, H * m : H * m + H],
                 start=True,
                 stop=True,
             )
-            hs = tile(H, BF16, "hs%d" % m)
+            hs[m] = tile(H, BF16, "hs%d" % m)
             nc.scalar.activation(
-                hs[:].rearrange("s (v p e) -> s v p e", v=2, e=2),
+                hs[m][:].rearrange("s (v p e) -> s v p e", v=2, e=2),
                 pre[:].rearrange("s (p v e) -> s v p e", v=2, e=2),
                 mybir.ActivationFunctionType.Silu,
             )
-            turned = psum.tile([P, 2, S], F32, name="turned", tag="turned", bufs=2)
-            for v in range(2):
-                nc.tensor.transpose(turned[:, v, :], hs[:].bitcast(F32)[:, P * v : P * v + P], ident[:])
-            hT[m] = tile(4 * S, BF16, "hT%d" % m)
-            nc.scalar.copy(
-                hT[m][:].bitcast(F32).rearrange("p (s v) -> p s v", v=2),
-                turned[:].rearrange("p v s -> p s v"),
-            )
 
-        def second_layer(m, over="", parts=1):
+        def turn(blocks, bank):
+            turned = psum.tile([P, len(blocks), 2, S], F32, name="turned", tag=bank)
+            for n, m in enumerate(blocks):
+                for v in range(2):
+                    nc.tensor.transpose(turned[:, n, v, :], hs[m][:].bitcast(F32)[:, P * v : P * v + P], ident[:])
+            for n, m in enumerate(blocks):
+                hT[m] = tile(PACK * S, BF16, "hT%d" % m)
+                nc.scalar.copy(
+                    hT[m][:].bitcast(F32).rearrange("p (s v) -> p s v", v=2),
+                    turned[:, n].rearrange("p v s -> p s v"),
+                )
+
+        def second_layer(m, hq_over="", y_over=""):
             j, u = divmod(m, 2)
-            hq[m] = tile(S, I32, "hq%d" % m, over)
-            hqs[m] = tile(S, U8, "hqs%d" % m)
-            nc.vector.quantize_mx(out=hq[m][:].bitcast(FP8X4), scales=hqs[m][:], in_=hT[m][:])
-            acc = psum.tile([P, 2, S], F32, name="acc", tag="acc", bufs=3)
-            for a in range(2):
+            hq = tile(S, I32, "hq%d" % m, hq_over)
+            hqs = tile(S, U8, "hqs%d" % m)
+            nc.vector.quantize_mx(out=hq[:].bitcast(FP8X4), scales=hqs[:], in_=hT[m][:])
+            acc = psum.tile([P, HALVES, S], F32, name="acc", tag="acc%d" % m)
+            for a in range(HALVES):
                 c = N * u + P * a
                 nc.tensor.matmul_mx(
                     out=acc[:, a, :],
-                    lhsT=w2w[j][:, c : c + P].bitcast(FP8X4),
+                    lhsT=w2w[m][:, P * a : P * a + P].bitcast(FP8X4),
                     lhsT_scale=w2s[j][W2_ROW:, c : c + P],
-                    rhs=hq[m][:].bitcast(FP8X4),
-                    rhs_scale=hqs[m][:],
+                    rhs=hq[:].bitcast(FP8X4),
+                    rhs_scale=hqs[:],
                     start=True,
                     stop=True,
                 )
-            if parts == 1:
-                both = tile(2 * S, F32, "y%d" % m)
-                nc.scalar.copy(both[:], acc[:].rearrange("p a s -> p (a s)"))
-                y[m] = [both[:, S * a : S * a + S] for a in range(2)]
-            else:
-                halves = [tile(S, F32, "y%d_%d" % (m, a)) for a in range(2)]
-                for a in range(2):
-                    nc.scalar.copy(halves[a][:], acc[:, a, :])
-                y[m] = [half[:] for half in halves]
+            y[m] = tile(HALVES * S, F32, "y%d" % m, y_over)
+            nc.scalar.copy(y[m][:], acc[:].rearrange("p a s -> p (a s)"))
 
         def scatter(m):
-            for a in range(2):
+            for a in range(HALVES):
                 nc.vector.tensor_tensor(
-                    res[a][:].indirect(tok[:, 8 * m : 8 * m + 8]),
-                    y[m][a],
+                    res[a][:].indirect(entries(tok, S * m, S * m + S)),
+                    y[m][:, S * a : S * a + S],
                     g[:, S * m : S * m + S],
                     mybir.AluOpType.mult,
                 )
 
-        xw = [gather_words(xw_all, tok, 256 * j, 256 * j + 256, "xw%d" % j) for j in range(2)]
+        xw = [gather_words(xw_all, tok, PAIR * j, PAIR * j + PAIR, "xw%d" % j) for j in range(2)]
         w1s = gather_scales(w1s_all, col1, 0, B * H, "w1s")
         permute_scales(0)
         permute_scales(1)
-        xs = [gather_scales(xs_all, tok, 256 * j, 256 * j + 256, "xs%d" % j) for j in range(2)]
-        gather_w1(0)
-        first_layer(0)
-        gather_w1(1)
-        first_layer(1)
+        xs = [gather_scales(xs_all, tok, PAIR * j, PAIR * j + PAIR, "xs%d" % j) for j in range(2)]
+
+        first_layer_direct(0)
+        first_layer_direct(1)
         first_layer_turned(2)
         first_layer_turned(3)
+
         w2s = [gather_scales(w2s_all, col2, 0, 2 * N, "w2s0")]
-        w2w = [gather_words(w2w_all, col2, 2 * N * j, 2 * N * j + 2 * N, "w2w%d" % j) for j in range(2)]
-        second_layer(0, parts=2)
-        second_layer(1, over="hq0")
-        w2s.append(gather_scales(w2s_all, col2, 2 * N, 4 * N, "w2s1", over="hqs0"))
+        w2w_first = gather_words(w2w_all, col2, 0, N, "w2w_first")
+        w2w_rest = gather_words(w2w_all, col2, N, B * N, "w2w_rest")
+        w2w = [w2w_first[:]] + [w2w_rest[:, N * m : N * m + N] for m in range(B - 1)]
+        second_layer(0)
+        turn((2, 3), "acc0")
+        second_layer(1, hq_over="hq0", y_over="hs3")
+        w2s.append(gather_scales(w2s_all, col2, 2 * N, B * N, "w2s1", over="hqs0"))
         scatter(0)
-        second_layer(2, over="hT1")
-        second_layer(3, over="y0_0")
-        scatter(1)
-        scatter(2)
-        scatter(3)
-        for a in range(2):
+        second_layer(2)
+        second_layer(3)
+        for m in range(1, B):
+            scatter(m)
+        for a in range(HALVES):
             nc.sync.dma_start(out[P * a : P * a + P, :], res[a][:])

@@ -42,9 +42,9 @@ def tile_moe_dyn_silu_kernel(
             nc.sync.dma_start(t[:], src)
             return t
 
-        def load_words(src, name):
+        def load_words(queue, src, name):
             t = tile(src.shape[2], I32, name)
-            nc.sync.dma_start(t[:], words_of(src))
+            queue.dma_start(t[:], words_of(src))
             return t
 
         def load_scales(t, src, row):
@@ -64,10 +64,11 @@ def tile_moe_dyn_silu_kernel(
             nc.vector.tensor_copy(t[:], table[:].indirect(entries(lst, a, b)))
             return t
 
-        xs_all = tile(T, U8, "xs_all")
-        nc.gpsimd.memset(xs_all[:].bitcast(I32), 0)
         w1s_all = tile(E * H, U8, "w1s_all")
-        nc.vector.memset(w1s_all[:].bitcast(I32), 0)
+        nc.gpsimd.memset(w1s_all[:, : E * H // 2].bitcast(I32), 0)
+        nc.vector.memset(w1s_all[:, E * H // 2 :].bitcast(I32), 0)
+        xs_all = tile(T, U8, "xs_all")
+        nc.vector.memset(xs_all[:].bitcast(I32), 0)
         w2s_all = tile(E * N, U8, "w2s_all")
         nc.vector.memset(w2s_all[:].bitcast(I32), 0)
         ident = keep.tile([P, P], F32, name="ident")
@@ -75,7 +76,7 @@ def tile_moe_dyn_silu_kernel(
         make_identity(nc, ident[:], nomemset=True)
 
         tok = load_list(offs, "tok")
-        xw_all = load_words(x_words, "xw_all")
+        xw_all = load_words(nc.scalar, x_words, "xw_all")
         col1 = load_list(offs2, "col1")
         w1w_all = tile(E * H, I32, "w1w_all")
         half = E * H // 2
@@ -85,7 +86,7 @@ def tile_moe_dyn_silu_kernel(
         nc.sync.dma_start(w1w_all[:, half:], words_of(w1_words)[:, half:])
         col2 = load_list(offs3, "col2")
         load_scales(w2s_all, w2_scales, W2_ROW)
-        w2w_all = load_words(w2_words, "w2w_all")
+        w2w_all = load_words(nc.sync, w2_words, "w2w_all")
         g = tile(S * B, F32, "g")
         nc.sync.dma_start(g[:], gate)
 
@@ -101,7 +102,7 @@ def tile_moe_dyn_silu_kernel(
             w1p[m] = tile(H, U8, "w1p%d" % m)
             nc.vector.tensor_copy(
                 w1p[m][:].rearrange("p (t c) -> p t c", t=PACK),
-                w1s[:, H * m : H * m + H].rearrange("p (c t) -> p t c", t=PACK),
+                w1s[0][:, H * m : H * m + H].rearrange("p (c t) -> p t c", t=PACK),
             )
 
         def first_layer_direct(m):
@@ -138,7 +139,7 @@ def tile_moe_dyn_silu_kernel(
                 lhsT=codes,
                 lhsT_scale=scales,
                 rhs=w1w[:].bitcast(FP8X4),
-                rhs_scale=w1s[W1_ROW:, H * m : H * m + H],
+                rhs_scale=w1s[1][W1_ROW:, H * (m % 2) : H * (m % 2) + H],
                 start=True,
                 stop=True,
             )
@@ -191,7 +192,7 @@ def tile_moe_dyn_silu_kernel(
                 )
 
         xw = [gather_words(xw_all, tok, PAIR * j, PAIR * j + PAIR, "xw%d" % j) for j in range(2)]
-        w1s = gather_scales(w1s_all, col1, 0, B * H, "w1s")
+        w1s = [gather_scales(w1s_all, col1, 2 * H * j, 2 * H * j + 2 * H, "w1s%d" % j) for j in range(2)]
         permute_scales(0)
         permute_scales(1)
         xs = [gather_scales(xs_all, tok, PAIR * j, PAIR * j + PAIR, "xs%d" % j) for j in range(2)]

@@ -18,7 +18,7 @@ P = 128
 S = 128
 PACK = 4
 LIST = 16
-PAIR = 2 * S
+WIDE = T + 192
 HALVES = N // P
 X_ROW, W1_ROW, W2_ROW = 0, 4, 8
 
@@ -42,20 +42,20 @@ def tile_moe_dyn_silu_kernel(
             nc.sync.dma_start(t[:], src)
             return t
 
-        def load_words(queue, src, name):
-            t = tile(src.shape[2], I32, name)
-            queue.dma_start(t[:], words_of(src))
+        def load_words(queue, src, name, width):
+            t = tile(width, I32, name)
+            queue.dma_start(t[:, : src.shape[2]], words_of(src))
             return t
 
         def load_scales(t, src, row):
             for q in range(4):
-                nc.sync.dma_start(t[row + q : P : 32, :].bitcast(I32), src[0, q:16:4, :].bitcast(I32))
+                nc.sync.dma_start(t[row + q : P : 32, : src.shape[2]].bitcast(I32), src[0, q:16:4, :].bitcast(I32))
 
         def entries(lst, a, b):
             return lst[:, a // LIST : b // LIST]
 
-        def gather_words(table, lst, a, b, name):
-            t = tile(b - a, I32, name)
+        def gather_words(table, lst, a, b, name, over=""):
+            t = tile(b - a, I32, name, over)
             nc.vector.tensor_copy(t[:].bitcast(U32), table[:].bitcast(U32).indirect(entries(lst, a, b)))
             return t
 
@@ -67,7 +67,7 @@ def tile_moe_dyn_silu_kernel(
         w1s_all = tile(E * H, U8, "w1s_all")
         nc.gpsimd.memset(w1s_all[:, : E * H // 2].bitcast(I32), 0)
         nc.vector.memset(w1s_all[:, E * H // 2 :].bitcast(I32), 0)
-        xs_all = tile(T, U8, "xs_all")
+        xs_all = tile(WIDE, U8, "xs_all")
         nc.vector.memset(xs_all[:].bitcast(I32), 0)
         w2s_all = tile(E * N, U8, "w2s_all")
         nc.vector.memset(w2s_all[:].bitcast(I32), 0)
@@ -76,34 +76,35 @@ def tile_moe_dyn_silu_kernel(
         make_identity(nc, ident[:], nomemset=True)
 
         tok = load_list(offs, "tok")
-        xw_all = load_words(nc.scalar, x_words, "xw_all")
+        xw_all = load_words(nc.scalar, x_words, "xw_all", WIDE)
         col1 = load_list(offs2, "col1")
         w1w_all = tile(E * H, I32, "w1w_all")
-        half = E * H // 2
+        cut1, cut2 = 1280, 3072
         load_scales(w1s_all, w1_scales, W1_ROW)
-        nc.sync.dma_start(w1w_all[:, :half], words_of(w1_words)[:, :half])
+        nc.sync.dma_start(w1w_all[:, :cut1], words_of(w1_words)[:, :cut1])
         load_scales(xs_all, x_scales, X_ROW)
-        nc.sync.dma_start(w1w_all[:, half:], words_of(w1_words)[:, half:])
+        nc.sync.dma_start(w1w_all[:, cut1:cut2], words_of(w1_words)[:, cut1:cut2])
         col2 = load_list(offs3, "col2")
         load_scales(w2s_all, w2_scales, W2_ROW)
-        w2w_all = load_words(nc.sync, w2_words, "w2w_all")
+        nc.sync.dma_start(w1w_all[:, cut2:], words_of(w1_words)[:, cut2:])
+        w2w_all = load_words(nc.sync, w2_words, "w2w_all", E * N)
         g = tile(S * B, F32, "g")
         nc.sync.dma_start(g[:], gate)
 
-        w1p, hs, hT, y = {}, {}, {}, {}
+        pres, hs, hT, quantised, y = {}, {}, {}, {}, {}
         res = [keep.tile([P, T], F32, name="res%d" % a) for a in range(HALVES)]
 
         def slots(m):
-            j, u = divmod(m, 2)
-            cols = slice(S * u, S * u + S)
-            return xw[j][:, cols].bitcast(FP8X4), xs[j][X_ROW:, cols]
+            cols = slice(S * m, S * m + S)
+            return xw[:, cols].bitcast(FP8X4), xs[X_ROW:, cols]
 
-        def permute_scales(m):
-            w1p[m] = tile(H, U8, "w1p%d" % m)
+        def permute_scales():
+            t = tile(2 * H, U8, "w1p")
             nc.vector.tensor_copy(
-                w1p[m][:].rearrange("p (t c) -> p t c", t=PACK),
-                w1s[0][:, H * m : H * m + H].rearrange("p (c t) -> p t c", t=PACK),
+                t[:].rearrange("p (m t c) -> p m t c", m=2, t=PACK),
+                w1s[0][:].rearrange("p (m c t) -> p m t c", m=2, t=PACK),
             )
+            return t
 
         def first_layer_direct(m):
             w1w = tile(H, I32, "w1w%d" % m)
@@ -117,7 +118,7 @@ def tile_moe_dyn_silu_kernel(
                 nc.tensor.matmul_mx(
                     out=pre[:, t, :],
                     lhsT=w1w[:, P * t : P * t + P].bitcast(FP8X4),
-                    lhsT_scale=w1p[m][W1_ROW:, P * t : P * t + P],
+                    lhsT_scale=w1p[W1_ROW:, H * m + P * t : H * m + P * t + P],
                     rhs=codes,
                     rhs_scale=scales,
                     start=True,
@@ -143,77 +144,103 @@ def tile_moe_dyn_silu_kernel(
                 start=True,
                 stop=True,
             )
-            hs[m] = tile(H, BF16, "hs%d" % m)
+            pres[m] = pre
+
+        def silu_turned(m, over=""):
+            hs[m] = tile(H, BF16, "hs%d" % m, over)
             nc.scalar.activation(
                 hs[m][:].rearrange("s (v p e) -> s v p e", v=2, e=2),
-                pre[:].rearrange("s (p v e) -> s v p e", v=2, e=2),
+                pres[m][:].rearrange("s (p v e) -> s v p e", v=2, e=2),
                 mybir.ActivationFunctionType.Silu,
             )
 
-        def turn(blocks, bank):
-            turned = psum.tile([P, len(blocks), 2, S], F32, name="turned", tag=bank)
-            for n, m in enumerate(blocks):
-                for v in range(2):
-                    nc.tensor.transpose(turned[:, n, v, :], hs[m][:].bitcast(F32)[:, P * v : P * v + P], ident[:])
-            for n, m in enumerate(blocks):
-                hT[m] = tile(PACK * S, BF16, "hT%d" % m)
-                nc.scalar.copy(
-                    hT[m][:].bitcast(F32).rearrange("p (s v) -> p s v", v=2),
-                    turned[:, n].rearrange("p v s -> p s v"),
-                )
+        def turn(m, bank, bufs=1):
+            turned = psum.tile([P, 2, S], F32, name="turned", tag=bank, bufs=bufs)
+            for v in range(2):
+                nc.tensor.transpose(turned[:, v, :], hs[m][:].bitcast(F32)[:, P * v : P * v + P], ident[:])
+            hT[m] = tile(PACK * S, BF16, "hT%d" % m)
+            nc.scalar.copy(
+                hT[m][:].bitcast(F32).rearrange("p (s v) -> p s v", v=2),
+                turned[:].rearrange("p v s -> p s v"),
+            )
 
-        def second_layer(m, hq_over="", y_over=""):
-            j, u = divmod(m, 2)
-            hq = tile(S, I32, "hq%d" % m, hq_over)
+        def quantise(m, over=""):
+            hq = tile(S, I32, "hq%d" % m, over)
             hqs = tile(S, U8, "hqs%d" % m)
             nc.vector.quantize_mx(out=hq[:].bitcast(FP8X4), scales=hqs[:], in_=hT[m][:])
+            quantised[m] = hq, hqs
+
+        def second_layer(m):
+            hq, hqs = quantised[m]
             acc = psum.tile([P, HALVES, S], F32, name="acc", tag="acc%d" % m)
             for a in range(HALVES):
-                c = N * u + P * a
+                c = N * m + P * a
                 nc.tensor.matmul_mx(
                     out=acc[:, a, :],
                     lhsT=w2w[m][:, P * a : P * a + P].bitcast(FP8X4),
-                    lhsT_scale=w2s[j][W2_ROW:, c : c + P],
+                    lhsT_scale=w2s[W2_ROW:, c : c + P],
                     rhs=hq[:].bitcast(FP8X4),
                     rhs_scale=hqs[:],
                     start=True,
                     stop=True,
                 )
-            y[m] = tile(HALVES * S, F32, "y%d" % m, y_over)
-            nc.scalar.copy(y[m][:], acc[:].rearrange("p a s -> p (a s)"))
+            return acc
 
-        def scatter(m):
+        def copy_out(m, acc):
+            t = tile(HALVES * S, F32, "y%d" % m)
+            nc.scalar.copy(t[:], acc[:].rearrange("p a s -> p (a s)"))
             for a in range(HALVES):
-                nc.vector.tensor_tensor(
-                    res[a][:].indirect(entries(tok, S * m, S * m + S)),
-                    y[m][:, S * a : S * a + S],
-                    g[:, S * m : S * m + S],
-                    mybir.AluOpType.mult,
-                )
+                y[m, a] = t[:, S * a : S * a + S]
 
-        xw = [gather_words(xw_all, tok, PAIR * j, PAIR * j + PAIR, "xw%d" % j) for j in range(2)]
+        def copy_half(m, a, acc, over=""):
+            t = tile(S, F32, "y%d_%d" % (m, a), over)
+            nc.scalar.copy(t[:], acc[:, a, :])
+            y[m, a] = t[:]
+
+        def scatter(m, a):
+            nc.vector.tensor_tensor(
+                res[a][:].indirect(entries(tok, S * m, S * m + S)),
+                y[m, a],
+                g[:, S * m : S * m + S],
+                mybir.AluOpType.mult,
+            )
+
+        xw = gather_words(xw_all, tok, 0, T, "xw")
         w1s = [gather_scales(w1s_all, col1, 2 * H * j, 2 * H * j + 2 * H, "w1s%d" % j) for j in range(2)]
-        permute_scales(0)
-        permute_scales(1)
-        xs = [gather_scales(xs_all, tok, PAIR * j, PAIR * j + PAIR, "xs%d" % j) for j in range(2)]
+        w1p = permute_scales()
+        xs = gather_scales(xs_all, tok, 0, T, "xs")
+        w2s = gather_scales(w2s_all, col2, 0, B * N, "w2s")
 
         first_layer_direct(0)
         first_layer_direct(1)
         first_layer_turned(2)
+        silu_turned(2)
         first_layer_turned(3)
 
-        w2s = [gather_scales(w2s_all, col2, 0, 2 * N, "w2s0")]
+        quantise(0)
         w2w_first = gather_words(w2w_all, col2, 0, N, "w2w_first")
-        w2w_rest = gather_words(w2w_all, col2, N, B * N, "w2w_rest")
+        w2w_rest = gather_words(w2w_all, col2, N, B * N, "w2w_rest", over="hT0")
         w2w = [w2w_first[:]] + [w2w_rest[:, N * m : N * m + N] for m in range(B - 1)]
-        second_layer(0)
-        turn((2, 3), "acc0")
-        second_layer(1, hq_over="hq0", y_over="hs3")
-        w2s.append(gather_scales(w2s_all, col2, 2 * N, B * N, "w2s1", over="hqs0"))
-        scatter(0)
-        second_layer(2)
-        second_layer(3)
-        for m in range(1, B):
-            scatter(m)
+        copy_out(0, second_layer(0))
+        silu_turned(3, over="w2w_first")
+        quantise(1, over="hq0")
+        acc1 = second_layer(1)
+        copy_half(1, 0, acc1)
+        turn(2, "acc0")
+        turn(3, "pre", B)
+        scatter(0, 0)
+        scatter(0, 1)
+        scatter(1, 0)
+        quantise(2)
+        acc2 = second_layer(2)
+        quantise(3)
+        acc3 = second_layer(3)
+        copy_half(1, 1, acc1, over="w2w_first")
+        scatter(1, 1)
+        copy_out(2, acc2)
+        copy_out(3, acc3)
+        for m in range(2, B):
+            for a in range(HALVES):
+                scatter(m, a)
         for a in range(HALVES):
             nc.sync.dma_start(out[P * a : P * a + P, :], res[a][:])

@@ -21,6 +21,7 @@ LIST = 16
 WIDE = T + 192
 HALVES = N // P
 X_ROW, W1_ROW, W2_ROW = 0, 4, 8
+STAGE = P - 16
 
 
 def tile_moe_dyn_silu_kernel(
@@ -42,8 +43,8 @@ def tile_moe_dyn_silu_kernel(
             nc.sync.dma_start(t[:], src)
             return t
 
-        def load_words(queue, src, name, width):
-            t = tile(width, I32, name)
+        def load_words(queue, src, name, width, over=""):
+            t = tile(width, I32, name, over)
             queue.dma_start(t[:, : src.shape[2]], words_of(src))
             return t
 
@@ -65,31 +66,28 @@ def tile_moe_dyn_silu_kernel(
             return t
 
         w1s_all = tile(E * H, U8, "w1s_all")
-        nc.gpsimd.memset(w1s_all[:, : E * H // 2].bitcast(I32), 0)
-        nc.vector.memset(w1s_all[:, E * H // 2 :].bitcast(I32), 0)
+        nc.vector.memset(w1s_all[:].bitcast(I32), 0)
+        w2s_all = tile(E * N, U8, "w2s_all")
+        nc.gpsimd.memset(w2s_all[:STAGE, :].bitcast(I32), 0)
+        w2s = tile(B * N, U8, "w2s")
+        nc.vector.memset(w2s[:].bitcast(I32), 0)
         xs_all = tile(WIDE, U8, "xs_all")
         nc.vector.memset(xs_all[:].bitcast(I32), 0)
-        w2s_all = tile(E * N, U8, "w2s_all")
-        nc.vector.memset(w2s_all[:].bitcast(I32), 0)
         ident = keep.tile([P, P], F32, name="ident")
         nc.vector.memset(ident[:], 0.0)
         make_identity(nc, ident[:], nomemset=True)
 
+        col2 = load_list(offs3, "col2")
+        nc.scalar.dma_start(w2s_all[STAGE:, :].bitcast(I32), w2_scales[0].bitcast(I32))
         tok = load_list(offs, "tok")
-        xw_all = load_words(nc.scalar, x_words, "xw_all", WIDE)
+        xw_all = load_words(nc.sync, x_words, "xw_all", WIDE)
+        load_scales(w1s_all, w1_scales, W1_ROW)
         col1 = load_list(offs2, "col1")
         w1w_all = tile(E * H, I32, "w1w_all")
-        cut1, cut2 = 1280, 3072
-        load_scales(w1s_all, w1_scales, W1_ROW)
-        nc.sync.dma_start(w1w_all[:, :cut1], words_of(w1_words)[:, :cut1])
+        half = E * H // 2
+        nc.sync.dma_start(w1w_all[:, :half], words_of(w1_words)[:, :half])
         load_scales(xs_all, x_scales, X_ROW)
-        nc.sync.dma_start(w1w_all[:, cut1:cut2], words_of(w1_words)[:, cut1:cut2])
-        col2 = load_list(offs3, "col2")
-        load_scales(w2s_all, w2_scales, W2_ROW)
-        nc.sync.dma_start(w1w_all[:, cut2:], words_of(w1_words)[:, cut2:])
-        w2w_all = load_words(nc.sync, w2_words, "w2w_all", E * N)
-        g = tile(S * B, F32, "g")
-        nc.sync.dma_start(g[:], gate)
+        nc.sync.dma_start(w1w_all[:, half:], words_of(w1_words)[:, half:])
 
         pres, hs, hT, quantised, y = {}, {}, {}, {}, {}
         res = [keep.tile([P, T], F32, name="res%d" % a) for a in range(HALVES)]
@@ -205,11 +203,16 @@ def tile_moe_dyn_silu_kernel(
                 mybir.AluOpType.mult,
             )
 
+        w2s_staged = gather_scales(w2s_all, col2, 0, B * N, "w2s_staged")
         xw = gather_words(xw_all, tok, 0, T, "xw")
+        for q in range(4):
+            nc.sync.dma_start(w2s[W2_ROW + q : P : 32, :].bitcast(I32), w2s_staged[STAGE + q : P : 4, :].bitcast(I32))
+        w2w_all = load_words(nc.sync, w2_words, "w2w_all", E * N, over="w2s_all")
         w1s = [gather_scales(w1s_all, col1, 2 * H * j, 2 * H * j + 2 * H, "w1s%d" % j) for j in range(2)]
+        g = tile(S * B, F32, "g", over="w1s_all")
+        nc.sync.dma_start(g[:], gate)
         w1p = permute_scales()
         xs = gather_scales(xs_all, tok, 0, T, "xs")
-        w2s = gather_scales(w2s_all, col2, 0, B * N, "w2s")
 
         first_layer_direct(0)
         first_layer_direct(1)
@@ -219,7 +222,7 @@ def tile_moe_dyn_silu_kernel(
 
         quantise(0)
         w2w_first = gather_words(w2w_all, col2, 0, N, "w2w_first")
-        w2w_rest = gather_words(w2w_all, col2, N, B * N, "w2w_rest", over="hT0")
+        w2w_rest = gather_words(w2w_all, col2, N, B * N, "w2w_rest")
         w2w = [w2w_first[:]] + [w2w_rest[:, N * m : N * m + N] for m in range(B - 1)]
         copy_out(0, second_layer(0))
         silu_turned(3, over="w2w_first")

@@ -43,9 +43,9 @@ def tile_moe_dyn_silu_kernel(
             nc.sync.dma_start(t[:], src)
             return t
 
-        def load_words(queue, src, name, width, over=""):
+        def load_words(src, name, width, over=""):
             t = tile(width, I32, name, over)
-            queue.dma_start(t[:, : src.shape[2]], words_of(src))
+            nc.sync.dma_start(t[:, : src.shape[2]], words_of(src))
             return t
 
         def load_scales(t, src, row):
@@ -55,13 +55,13 @@ def tile_moe_dyn_silu_kernel(
         def entries(lst, a, b):
             return lst[:, a // LIST : b // LIST]
 
-        def gather_words(table, lst, a, b, name, over=""):
-            t = tile(b - a, I32, name, over)
+        def gather_words(table, lst, a, b, name):
+            t = tile(b - a, I32, name)
             nc.vector.tensor_copy(t[:].bitcast(U32), table[:].bitcast(U32).indirect(entries(lst, a, b)))
             return t
 
-        def gather_scales(table, lst, a, b, name, over=""):
-            t = tile(b - a, U8, name, over)
+        def gather_scales(table, lst, a, b, name):
+            t = tile(b - a, U8, name)
             nc.vector.tensor_copy(t[:], table[:].indirect(entries(lst, a, b)))
             return t
 
@@ -80,7 +80,7 @@ def tile_moe_dyn_silu_kernel(
         col2 = load_list(offs3, "col2")
         nc.scalar.dma_start(w2s_all[STAGE:, :].bitcast(I32), w2_scales[0].bitcast(I32))
         tok = load_list(offs, "tok")
-        xw_all = load_words(nc.sync, x_words, "xw_all", WIDE)
+        xw_all = load_words(x_words, "xw_all", WIDE)
         load_scales(w1s_all, w1_scales, W1_ROW)
         col1 = load_list(offs2, "col1")
         w1w_all = tile(E * H, I32, "w1w_all")
@@ -168,13 +168,13 @@ def tile_moe_dyn_silu_kernel(
             nc.vector.quantize_mx(out=hq[:].bitcast(FP8X4), scales=hqs[:], in_=hT[m][:])
             quantised[m] = hq, hqs
 
-        def second_layer(m):
+        def second_layer(m, halves, bank):
             hq, hqs = quantised[m]
-            acc = psum.tile([P, HALVES, S], F32, name="acc", tag="acc%d" % m)
-            for a in range(HALVES):
+            acc = psum.tile([P, len(halves), S], F32, name="acc", tag=bank)
+            for n, a in enumerate(halves):
                 c = N * m + P * a
                 nc.tensor.matmul_mx(
-                    out=acc[:, a, :],
+                    out=acc[:, n, :],
                     lhsT=w2w[m][:, P * a : P * a + P].bitcast(FP8X4),
                     lhsT_scale=w2s[W2_ROW:, c : c + P],
                     rhs=hq[:].bitcast(FP8X4),
@@ -184,16 +184,11 @@ def tile_moe_dyn_silu_kernel(
                 )
             return acc
 
-        def copy_out(m, acc):
-            t = tile(HALVES * S, F32, "y%d" % m)
+        def copy_out(m, halves, acc):
+            t = tile(len(halves) * S, F32, "y%d_%d" % (m, halves[0]))
             nc.scalar.copy(t[:], acc[:].rearrange("p a s -> p (a s)"))
-            for a in range(HALVES):
-                y[m, a] = t[:, S * a : S * a + S]
-
-        def copy_half(m, a, acc, over=""):
-            t = tile(S, F32, "y%d_%d" % (m, a), over)
-            nc.scalar.copy(t[:], acc[:, a, :])
-            y[m, a] = t[:]
+            for n, a in enumerate(halves):
+                y[m, a] = t[:, S * n : S * n + S]
 
         def scatter(m, a):
             nc.vector.tensor_tensor(
@@ -207,7 +202,7 @@ def tile_moe_dyn_silu_kernel(
         xw = gather_words(xw_all, tok, 0, T, "xw")
         for q in range(4):
             nc.sync.dma_start(w2s[W2_ROW + q : P : 32, :].bitcast(I32), w2s_staged[STAGE + q : P : 4, :].bitcast(I32))
-        w2w_all = load_words(nc.sync, w2_words, "w2w_all", E * N, over="w2s_all")
+        w2w_all = load_words(w2_words, "w2w_all", E * N, over="w2s_all")
         w1s = [gather_scales(w1s_all, col1, 2 * H * j, 2 * H * j + 2 * H, "w1s%d" % j) for j in range(2)]
         g = tile(S * B, F32, "g", over="w1s_all")
         nc.sync.dma_start(g[:], gate)
@@ -224,26 +219,20 @@ def tile_moe_dyn_silu_kernel(
         w2w_first = gather_words(w2w_all, col2, 0, N, "w2w_first")
         w2w_rest = gather_words(w2w_all, col2, N, B * N, "w2w_rest")
         w2w = [w2w_first[:]] + [w2w_rest[:, N * m : N * m + N] for m in range(B - 1)]
-        copy_out(0, second_layer(0))
+        both = tuple(range(HALVES))
+        acc0 = [second_layer(0, (a,), "acc0_%d" % a) for a in both]
+        for a in both:
+            copy_out(0, (a,), acc0[a])
         silu_turned(3, over="w2w_first")
         quantise(1, over="hq0")
-        acc1 = second_layer(1)
-        copy_half(1, 0, acc1)
-        turn(2, "acc0")
+        turn(2, "acc0_0")
+        copy_out(1, both, second_layer(1, both, "acc0_1"))
         turn(3, "pre", B)
-        scatter(0, 0)
-        scatter(0, 1)
-        scatter(1, 0)
-        quantise(2)
-        acc2 = second_layer(2)
-        quantise(3)
-        acc3 = second_layer(3)
-        copy_half(1, 1, acc1, over="w2w_first")
-        scatter(1, 1)
-        copy_out(2, acc2)
-        copy_out(3, acc3)
-        for m in range(2, B):
-            for a in range(HALVES):
+        for m in range(B):
+            for a in both:
                 scatter(m, a)
-        for a in range(HALVES):
+            if m + 2 < B:
+                quantise(m + 2)
+                copy_out(m + 2, both, second_layer(m + 2, both, "acc%d" % (m + 2)))
+        for a in both:
             nc.sync.dma_start(out[P * a : P * a + P, :], res[a][:])

@@ -1,7 +1,6 @@
 from contextlib import ExitStack
 
 import concourse.mybir as mybir
-from concourse.masks import make_identity
 
 K, T, E, B, H, N = 512, 512, 8, 4, 512, 256
 FLOPS = 2 * 128 * B * (K * H + H * N)
@@ -55,8 +54,8 @@ def tile_moe_dyn_silu_kernel(
         def entries(lst, a, b):
             return lst[:, a // LIST : b // LIST]
 
-        def gather_words(table, lst, a, b, name):
-            t = tile(b - a, I32, name)
+        def gather_words(table, lst, a, b, name, over=""):
+            t = tile(b - a, I32, name, over)
             nc.vector.tensor_copy(t[:].bitcast(U32), table[:].bitcast(U32).indirect(entries(lst, a, b)))
             return t
 
@@ -73,9 +72,6 @@ def tile_moe_dyn_silu_kernel(
         nc.vector.memset(w2s[:].bitcast(I32), 0)
         xs_all = tile(WIDE, U8, "xs_all")
         nc.vector.memset(xs_all[:].bitcast(I32), 0)
-        ident = keep.tile([P, P], F32, name="ident")
-        nc.vector.memset(ident[:], 0.0)
-        make_identity(nc, ident[:], nomemset=True)
 
         col2 = load_list(offs3, "col2")
         nc.scalar.dma_start(w2s_all[STAGE:, :].bitcast(I32), w2_scales[0].bitcast(I32))
@@ -89,36 +85,33 @@ def tile_moe_dyn_silu_kernel(
         load_scales(xs_all, x_scales, X_ROW)
         nc.sync.dma_start(w1w_all[:, half:], words_of(w1_words)[:, half:])
 
-        pres, hs, hT, quantised, y = {}, {}, {}, {}, {}
+        hT, quantised, w2w, y = {}, {}, {}, {}
         res = [keep.tile([P, T], F32, name="res%d" % a) for a in range(HALVES)]
 
-        def slots(m):
-            cols = slice(S * m, S * m + S)
-            return xw[:, cols].bitcast(FP8X4), xs[X_ROW:, cols]
-
-        def permute_scales():
-            t = tile(2 * H, U8, "w1p")
+        def permute_scales(j):
+            t = tile(2 * H, U8, "w1p%d" % j)
             nc.vector.tensor_copy(
                 t[:].rearrange("p (m t c) -> p m t c", m=2, t=PACK),
-                w1s[0][:].rearrange("p (m c t) -> p m t c", m=2, t=PACK),
+                w1s[j][:].rearrange("p (m c t) -> p m t c", m=2, t=PACK),
             )
             return t
 
-        def first_layer_direct(m):
+        def first_layer(m):
             w1w = tile(H, I32, "w1w%d" % m)
             nc.vector.tensor_copy(
                 w1w[:].bitcast(U32).rearrange("p (t c) -> p c t", t=PACK),
                 w1w_all[:].bitcast(U32).indirect(entries(col1, H * m, H * m + H)),
             )
-            codes, scales = slots(m)
-            pre = psum.tile([P, PACK, S], F32, name="pre", tag="pre", bufs=B)
+            cols = slice(S * m, S * m + S)
+            pre = psum.tile([P, PACK, S], F32, name="pre%d" % m)
             for t in range(PACK):
+                c = H * (m % 2) + P * t
                 nc.tensor.matmul_mx(
                     out=pre[:, t, :],
                     lhsT=w1w[:, P * t : P * t + P].bitcast(FP8X4),
-                    lhsT_scale=w1p[W1_ROW:, H * m + P * t : H * m + P * t + P],
-                    rhs=codes,
-                    rhs_scale=scales,
+                    lhsT_scale=w1p[m // 2][W1_ROW:, c : c + P],
+                    rhs=xw[:, cols].bitcast(FP8X4),
+                    rhs_scale=xs[X_ROW:, cols],
                     start=True,
                     stop=True,
                 )
@@ -129,52 +122,19 @@ def tile_moe_dyn_silu_kernel(
                 mybir.ActivationFunctionType.Silu,
             )
 
-        def first_layer_turned(m):
-            w1w = gather_words(w1w_all, col1, H * m, H * m + H, "w1w%d" % m)
-            codes, scales = slots(m)
-            pre = psum.tile([P, H], F32, name="pre", tag="pre", bufs=B)
-            nc.tensor.matmul_mx(
-                out=pre[:],
-                lhsT=codes,
-                lhsT_scale=scales,
-                rhs=w1w[:].bitcast(FP8X4),
-                rhs_scale=w1s[1][W1_ROW:, H * (m % 2) : H * (m % 2) + H],
-                start=True,
-                stop=True,
-            )
-            pres[m] = pre
-
-        def silu_turned(m, over=""):
-            hs[m] = tile(H, BF16, "hs%d" % m, over)
-            nc.scalar.activation(
-                hs[m][:].rearrange("s (v p e) -> s v p e", v=2, e=2),
-                pres[m][:].rearrange("s (p v e) -> s v p e", v=2, e=2),
-                mybir.ActivationFunctionType.Silu,
-            )
-
-        def turn(m, bank, bufs=1):
-            turned = psum.tile([P, 2, S], F32, name="turned", tag=bank, bufs=bufs)
-            for v in range(2):
-                nc.tensor.transpose(turned[:, v, :], hs[m][:].bitcast(F32)[:, P * v : P * v + P], ident[:])
-            hT[m] = tile(PACK * S, BF16, "hT%d" % m)
-            nc.scalar.copy(
-                hT[m][:].bitcast(F32).rearrange("p (s v) -> p s v", v=2),
-                turned[:].rearrange("p v s -> p s v"),
-            )
-
-        def quantise(m, over=""):
-            hq = tile(S, I32, "hq%d" % m, over)
+        def quantise(m):
+            hq = tile(S, I32, "hq%d" % m, "hq%d" % (m % 2))
             hqs = tile(S, U8, "hqs%d" % m)
             nc.vector.quantize_mx(out=hq[:].bitcast(FP8X4), scales=hqs[:], in_=hT[m][:])
             quantised[m] = hq, hqs
 
-        def second_layer(m, halves, bank):
+        def second_layer(m):
             hq, hqs = quantised[m]
-            acc = psum.tile([P, len(halves), S], F32, name="acc", tag=bank)
-            for n, a in enumerate(halves):
+            acc = psum.tile([P, HALVES, S], F32, name="acc%d" % m)
+            for a in range(HALVES):
                 c = N * m + P * a
                 nc.tensor.matmul_mx(
-                    out=acc[:, n, :],
+                    out=acc[:, a, :],
                     lhsT=w2w[m][:, P * a : P * a + P].bitcast(FP8X4),
                     lhsT_scale=w2s[W2_ROW:, c : c + P],
                     rhs=hq[:].bitcast(FP8X4),
@@ -182,21 +142,20 @@ def tile_moe_dyn_silu_kernel(
                     start=True,
                     stop=True,
                 )
-            return acc
-
-        def copy_out(m, halves, acc):
-            t = tile(len(halves) * S, F32, "y%d_%d" % (m, halves[0]))
-            nc.scalar.copy(t[:], acc[:].rearrange("p a s -> p (a s)"))
-            for n, a in enumerate(halves):
-                y[m, a] = t[:, S * n : S * n + S]
-
-        def scatter(m, a):
+            y[m] = keep.tile([P, HALVES, S], F32, name="y%d" % m)
             nc.vector.tensor_tensor(
-                res[a][:].indirect(entries(tok, S * m, S * m + S)),
-                y[m, a],
-                g[:, S * m : S * m + S],
+                y[m][:],
+                acc[:],
+                g[:, S * m : S * m + S].unsqueeze(1).to_broadcast([P, HALVES, S]),
                 mybir.AluOpType.mult,
             )
+
+        def scatter(m, a, on_scalar):
+            window = res[a][:].indirect(entries(tok, S * m, S * m + S))
+            if on_scalar:
+                nc.scalar.activation(window, y[m][:, a, :], mybir.ActivationFunctionType.Copy)
+            else:
+                nc.vector.tensor_copy(window, y[m][:, a, :])
 
         w2s_staged = gather_scales(w2s_all, col2, 0, B * N, "w2s_staged")
         xw = gather_words(xw_all, tok, 0, T, "xw")
@@ -206,33 +165,21 @@ def tile_moe_dyn_silu_kernel(
         w1s = [gather_scales(w1s_all, col1, 2 * H * j, 2 * H * j + 2 * H, "w1s%d" % j) for j in range(2)]
         g = tile(S * B, F32, "g", over="w1s_all")
         nc.sync.dma_start(g[:], gate)
-        w1p = permute_scales()
+        w1p = [permute_scales(j) for j in range(2)]
         xs = gather_scales(xs_all, tok, 0, T, "xs")
 
-        first_layer_direct(0)
-        first_layer_direct(1)
-        first_layer_turned(2)
-        silu_turned(2)
-        first_layer_turned(3)
-
-        quantise(0)
-        w2w_first = gather_words(w2w_all, col2, 0, N, "w2w_first")
-        w2w_rest = gather_words(w2w_all, col2, N, B * N, "w2w_rest")
-        w2w = [w2w_first[:]] + [w2w_rest[:, N * m : N * m + N] for m in range(B - 1)]
-        both = tuple(range(HALVES))
-        acc0 = [second_layer(0, (a,), "acc0_%d" % a) for a in both]
-        for a in both:
-            copy_out(0, (a,), acc0[a])
-        silu_turned(3, over="w2w_first")
-        quantise(1, over="hq0")
-        turn(2, "acc0_0")
-        copy_out(1, both, second_layer(1, both, "acc0_1"))
-        turn(3, "pre", B)
         for m in range(B):
-            for a in both:
-                scatter(m, a)
-            if m + 2 < B:
-                quantise(m + 2)
-                copy_out(m + 2, both, second_layer(m + 2, both, "acc%d" % (m + 2)))
-        for a in both:
+            first_layer(m)
+        for m in range(B + 2):
+            if m >= 2:
+                second_layer(m - 2)
+            if m < B:
+                quantise(m)
+                w2w[m] = gather_words(w2w_all, col2, N * m, N * m + N, "w2w%d" % m, "w2w%d" % (m % 2))
+        scatter(0, 0, True)
+        for m in range(B):
+            scatter(m, 1, True)
+        for m in range(1, B):
+            scatter(m, 0, False)
+        for a in range(HALVES):
             nc.sync.dma_start(out[P * a : P * a + P, :], res[a][:])

@@ -84,8 +84,12 @@ def tile_moe_dyn_silu_kernel(
         nc.sync.dma_start(w1w_all[:, :half], words_of(w1_words)[:, :half])
         load_scales(xs_all, x_scales, X_ROW)
         nc.sync.dma_start(w1w_all[:, half:], words_of(w1_words)[:, half:])
+        g = tile(S * B, F32, "g")
+        nc.sync.dma_start(g[:], gate)
+        w2w_all = load_words(w2_words, "w2w_all", E * N)
 
-        hT, quantised, w2w, y = {}, {}, {}, {}
+        hT, quantised, w2w = {}, {}, {}
+        y = keep.tile([P, HALVES, T], F32, name="y")
         res = [keep.tile([P, T], F32, name="res%d" % a) for a in range(HALVES)]
 
         def permute_scales(j):
@@ -123,7 +127,7 @@ def tile_moe_dyn_silu_kernel(
             )
 
         def quantise(m):
-            hq = tile(S, I32, "hq%d" % m, "hq%d" % (m % 2))
+            hq = tile(S, I32, "hq%d" % m, "hq%d" % (m % 3))
             hqs = tile(S, U8, "hqs%d" % m)
             nc.vector.quantize_mx(out=hq[:].bitcast(FP8X4), scales=hqs[:], in_=hT[m][:])
             quantised[m] = hq, hqs
@@ -142,29 +146,26 @@ def tile_moe_dyn_silu_kernel(
                     start=True,
                     stop=True,
                 )
-            y[m] = keep.tile([P, HALVES, S], F32, name="y%d" % m)
             nc.vector.tensor_tensor(
-                y[m][:],
+                y[:, :, S * m : S * m + S],
                 acc[:],
                 g[:, S * m : S * m + S].unsqueeze(1).to_broadcast([P, HALVES, S]),
                 mybir.AluOpType.mult,
             )
 
-        def scatter(m, a, on_scalar):
-            window = res[a][:].indirect(entries(tok, S * m, S * m + S))
+        def scatter(a, first, last, on_scalar):
+            lo, hi = S * first, S * last + S
+            window = res[a][:].indirect(entries(tok, lo, hi))
             if on_scalar:
-                nc.scalar.activation(window, y[m][:, a, :], mybir.ActivationFunctionType.Copy)
+                nc.scalar.activation(window, y[:, a, lo:hi], mybir.ActivationFunctionType.Copy)
             else:
-                nc.vector.tensor_copy(window, y[m][:, a, :])
+                nc.vector.tensor_copy(window, y[:, a, lo:hi])
 
         w2s_staged = gather_scales(w2s_all, col2, 0, B * N, "w2s_staged")
         xw = gather_words(xw_all, tok, 0, T, "xw")
         for q in range(4):
             nc.sync.dma_start(w2s[W2_ROW + q : P : 32, :].bitcast(I32), w2s_staged[STAGE + q : P : 4, :].bitcast(I32))
-        w2w_all = load_words(w2_words, "w2w_all", E * N, over="w2s_all")
         w1s = [gather_scales(w1s_all, col1, 2 * H * j, 2 * H * j + 2 * H, "w1s%d" % j) for j in range(2)]
-        g = tile(S * B, F32, "g", over="w1s_all")
-        nc.sync.dma_start(g[:], gate)
         w1p = [permute_scales(j) for j in range(2)]
         xs = gather_scales(xs_all, tok, 0, T, "xs")
 
@@ -175,11 +176,11 @@ def tile_moe_dyn_silu_kernel(
                 second_layer(m - 2)
             if m < B:
                 quantise(m)
-                w2w[m] = gather_words(w2w_all, col2, N * m, N * m + N, "w2w%d" % m, "w2w%d" % (m % 2))
-        scatter(0, 0, True)
-        for m in range(B):
-            scatter(m, 1, True)
-        for m in range(1, B):
-            scatter(m, 0, False)
+                w2w[m] = gather_words(w2w_all, col2, N * m, N * m + N, "w2w%d" % m, ("w2w0", "hT0")[m % 2])
+        scatter(0, 0, 0, True)
+        scatter(1, 0, 1, True)
+        scatter(1, 2, 3, True)
+        scatter(0, 1, 1, False)
+        scatter(0, 2, 3, False)
         for a in range(HALVES):
             nc.sync.dma_start(out[P * a : P * a + P, :], res[a][:])

@@ -107,7 +107,7 @@ def tile_moe_dyn_silu_kernel(
                 w1w_all[:].bitcast(U32).indirect(entries(col1, H * m, H * m + H)),
             )
             cols = slice(S * m, S * m + S)
-            pre = psum.tile([P, PACK, S], F32, name="pre%d" % m)
+            pre = psum.tile([P, PACK, S], F32, name="pre%d" % m, tag="pre%d" % m)
             for t in range(PACK):
                 c = H * (m % 2) + P * t
                 nc.tensor.matmul_mx(
@@ -132,26 +132,24 @@ def tile_moe_dyn_silu_kernel(
             nc.vector.quantize_mx(out=hq[:].bitcast(FP8X4), scales=hqs[:], in_=hT[m][:])
             quantised[m] = hq, hqs
 
-        def second_layer(m):
+        def second_product(m, a, acc):
             hq, hqs = quantised[m]
-            acc = psum.tile([P, HALVES, S], F32, name="acc%d" % m)
-            for a in range(HALVES):
-                c = N * m + P * a
-                nc.tensor.matmul_mx(
-                    out=acc[:, a, :],
-                    lhsT=w2w[m][:, P * a : P * a + P].bitcast(FP8X4),
-                    lhsT_scale=w2s[W2_ROW:, c : c + P],
-                    rhs=hq[:].bitcast(FP8X4),
-                    rhs_scale=hqs[:],
-                    start=True,
-                    stop=True,
-                )
-            nc.vector.tensor_tensor(
-                y[:, :, S * m : S * m + S],
-                acc[:],
-                g[:, S * m : S * m + S].unsqueeze(1).to_broadcast([P, HALVES, S]),
-                mybir.AluOpType.mult,
+            c = N * m + P * a
+            nc.tensor.matmul_mx(
+                out=acc,
+                lhsT=w2w[m][:, P * a : P * a + P].bitcast(FP8X4),
+                lhsT_scale=w2s[W2_ROW:, c : c + P],
+                rhs=hq[:].bitcast(FP8X4),
+                rhs_scale=hqs[:],
+                start=True,
+                stop=True,
             )
+
+        def bank(name, tag):
+            return psum.tile([P, HALVES, S], F32, name=name, tag=tag)
+
+        def times_gate(acc, a, lo, hi):
+            nc.vector.tensor_tensor(y[:, a, lo:hi], acc, g[:, lo:hi], mybir.AluOpType.mult)
 
         def scatter(a, first, last, on_scalar):
             lo, hi = S * first, S * last + S
@@ -171,12 +169,33 @@ def tile_moe_dyn_silu_kernel(
 
         for m in range(B):
             first_layer(m)
-        for m in range(B + 2):
-            if m >= 2:
-                second_layer(m - 2)
-            if m < B:
-                quantise(m)
-                w2w[m] = gather_words(w2w_all, col2, N * m, N * m + N, "w2w%d" % m, ("w2w0", "hT0")[m % 2])
+        def operands(m):
+            quantise(m)
+            w2w[m] = gather_words(w2w_all, col2, N * m, N * m + N, "w2w%d" % m, ("w2w0", "hT0")[m % 2])
+
+        operands(0)
+        operands(1)
+        for a in range(HALVES):
+            acc = bank("acc0_%d" % a, "acc0_%d" % a)
+            second_product(0, a, acc[:, 0, :])
+            times_gate(acc[:, 0, :], a, 0, S)
+        operands(2)
+        acc = bank("acc1", "acc1")
+        for a in range(HALVES):
+            second_product(1, a, acc[:, a, :])
+        nc.vector.tensor_tensor(
+            y[:, :, S : 2 * S],
+            acc[:],
+            g[:, S : 2 * S].unsqueeze(1).to_broadcast([P, HALVES, S]),
+            mybir.AluOpType.mult,
+        )
+        operands(3)
+        late = [bank("late0", "late0"), bank("late1", "pre0")]
+        for m in (2, 3):
+            for a in range(HALVES):
+                second_product(m, a, late[a][:, m - 2, :])
+        for a in range(HALVES):
+            times_gate(late[a][:].rearrange("p m s -> p (m s)"), a, 2 * S, B * S)
         scatter(0, 0, 0, True)
         scatter(1, 0, 1, True)
         scatter(1, 2, 3, True)

@@ -1,6 +1,7 @@
 from contextlib import ExitStack
 
 import concourse.mybir as mybir
+from concourse.masks import make_identity
 
 K, T, E, B, H, N = 512, 512, 8, 4, 512, 256
 FLOPS = 2 * 128 * B * (K * H + H * N)
@@ -21,6 +22,7 @@ WIDE = T + 192
 HALVES = N // P
 X_ROW, W1_ROW, W2_ROW = 0, 4, 8
 STAGE = P - 16
+AHEAD = 2
 
 
 def tile_moe_dyn_silu_kernel(
@@ -72,6 +74,9 @@ def tile_moe_dyn_silu_kernel(
         nc.vector.memset(w2s[:].bitcast(I32), 0)
         xs_all = tile(WIDE, U8, "xs_all")
         nc.vector.memset(xs_all[:].bitcast(I32), 0)
+        ident = keep.tile([P, P], F32, name="ident")
+        nc.vector.memset(ident[:], 0.0)
+        make_identity(nc, ident[:], nomemset=True)
 
         col2 = load_list(offs3, "col2")
         nc.scalar.dma_start(w2s_all[STAGE:, :].bitcast(I32), w2_scales[0].bitcast(I32))
@@ -86,19 +91,49 @@ def tile_moe_dyn_silu_kernel(
         nc.sync.dma_start(w1w_all[:, half:], words_of(w1_words)[:, half:])
         g = tile(S * B, F32, "g")
         nc.sync.dma_start(g[:], gate)
-        w2w_all = load_words(w2_words, "w2w_all", E * N)
 
         hT, quantised, w2w = {}, {}, {}
         y = keep.tile([P, HALVES, T], F32, name="y")
         res = [keep.tile([P, T], F32, name="res%d" % a) for a in range(HALVES)]
 
-        def permute_scales(j):
-            t = tile(2 * H, U8, "w1p%d" % j)
+        def permute_scales(j, blocks):
+            t = tile(blocks * H, U8, "w1p%d" % j)
             nc.vector.tensor_copy(
-                t[:].rearrange("p (m t c) -> p m t c", m=2, t=PACK),
-                w1s[j][:].rearrange("p (m c t) -> p m t c", m=2, t=PACK),
+                t[:].rearrange("p (m t c) -> p m t c", m=blocks, t=PACK),
+                w1s[j][:, : blocks * H].rearrange("p (m c t) -> p m t c", m=blocks, t=PACK),
             )
             return t
+
+        def first_layer_turned(m):
+            w1w = gather_words(w1w_all, col1, H * m, H * m + H, "w1w%d" % m)
+            cols = slice(S * m, S * m + S)
+            pre = psum.tile([P, H], F32, name="pre%d" % m, tag="pre%d" % m)
+            nc.tensor.matmul_mx(
+                out=pre[:],
+                lhsT=xw[:, cols].bitcast(FP8X4),
+                lhsT_scale=xs[X_ROW:, cols],
+                rhs=w1w[:].bitcast(FP8X4),
+                rhs_scale=w1s[m // 2][W1_ROW:, H * (m % 2) : H * (m % 2) + H],
+                start=True,
+                stop=True,
+            )
+            hs = tile(H, BF16, "hs")
+            nc.scalar.activation(
+                hs[:].rearrange("s (v p e) -> s v p e", v=2, e=2),
+                pre[:].rearrange("s (p v e) -> s v p e", v=2, e=2),
+                mybir.ActivationFunctionType.Silu,
+            )
+            return hs
+
+        def turn(m, hs):
+            turned = psum.tile([P, 2, S], F32, name="turned")
+            for v in range(2):
+                nc.tensor.transpose(turned[:, v, :], hs[:].bitcast(F32)[:, P * v : P * v + P], ident[:])
+            hT[m] = tile(PACK * S, BF16, "hT%d" % m)
+            nc.scalar.copy(
+                hT[m][:].bitcast(F32).rearrange("p (s v) -> p s v", v=2),
+                turned[:].rearrange("p v s -> p s v"),
+            )
 
         def first_layer(m):
             w1w = tile(H, I32, "w1w%d" % m)
@@ -127,7 +162,7 @@ def tile_moe_dyn_silu_kernel(
             )
 
         def quantise(m):
-            hq = tile(S, I32, "hq%d" % m, "hq%d" % (m % 3))
+            hq = tile(S, I32, "hq%d" % m, "hq%d" % (m % 2))
             hqs = tile(S, U8, "hqs%d" % m)
             nc.vector.quantize_mx(out=hq[:].bitcast(FP8X4), scales=hqs[:], in_=hT[m][:])
             quantised[m] = hq, hqs
@@ -162,24 +197,31 @@ def tile_moe_dyn_silu_kernel(
         w2s_staged = gather_scales(w2s_all, col2, 0, B * N, "w2s_staged")
         xw = gather_words(xw_all, tok, 0, T, "xw")
         for q in range(4):
+            if q == AHEAD:
+                w2w_all = load_words(w2_words, "w2w_all", E * N, over="w2s_all")
             nc.sync.dma_start(w2s[W2_ROW + q : P : 32, :].bitcast(I32), w2s_staged[STAGE + q : P : 4, :].bitcast(I32))
         w1s = [gather_scales(w1s_all, col1, 2 * H * j, 2 * H * j + 2 * H, "w1s%d" % j) for j in range(2)]
-        w1p = [permute_scales(j) for j in range(2)]
+        w1p = [permute_scales(0, 2), permute_scales(1, 1)]
         xs = gather_scales(xs_all, tok, 0, T, "xs")
 
-        for m in range(B):
-            first_layer(m)
-        def operands(m):
-            quantise(m)
-            w2w[m] = gather_words(w2w_all, col2, N * m, N * m + N, "w2w%d" % m, ("w2w0", "hT0")[m % 2])
+        first_layer(0)
+        hs3 = first_layer_turned(3)
+        first_layer(1)
+        first_layer(2)
+        turn(3, hs3)
+        def second_words(m):
+            w2w[m] = gather_words(w2w_all, col2, N * m, N * m + N, "w2w%d" % m, "w2w%d" % (m % 3))
 
-        operands(0)
-        operands(1)
+        quantise(0)
+        for m in range(B - 1):
+            second_words(m)
+        quantise(1)
         for a in range(HALVES):
             acc = bank("acc0_%d" % a, "acc0_%d" % a)
             second_product(0, a, acc[:, 0, :])
             times_gate(acc[:, 0, :], a, 0, S)
-        operands(2)
+        second_words(3)
+        quantise(2)
         acc = bank("acc1", "acc1")
         for a in range(HALVES):
             second_product(1, a, acc[:, a, :])
@@ -189,8 +231,8 @@ def tile_moe_dyn_silu_kernel(
             g[:, S : 2 * S].unsqueeze(1).to_broadcast([P, HALVES, S]),
             mybir.AluOpType.mult,
         )
-        operands(3)
-        late = [bank("late0", "late0"), bank("late1", "pre0")]
+        quantise(3)
+        late = [bank("late0", "pre1"), bank("late1", "pre0")]
         for m in (2, 3):
             for a in range(HALVES):
                 second_product(m, a, late[a][:, m - 2, :])

@@ -22,6 +22,7 @@ WIDE = T + 192
 HALVES = N // P
 X_ROW, W1_ROW, W2_ROW = 0, 4, 8
 STAGE = P - 16
+LINE = 16
 AHEAD = 2
 
 
@@ -67,9 +68,10 @@ def tile_moe_dyn_silu_kernel(
             return t
 
         w1s_all = tile(E * H, U8, "w1s_all")
-        nc.vector.memset(w1s_all[:].bitcast(I32), 0)
+        nc.gpsimd.memset(w1s_all[:, : E * H // 2].bitcast(I32), 0)
+        nc.vector.memset(w1s_all[:, E * H // 2 :].bitcast(I32), 0)
         w2s_all = tile(E * N, U8, "w2s_all")
-        nc.gpsimd.memset(w2s_all[:STAGE, :].bitcast(I32), 0)
+        nc.vector.memset(w2s_all[:STAGE, :].bitcast(I32), 0)
         w2s = tile(B * N, U8, "w2s")
         nc.vector.memset(w2s[:].bitcast(I32), 0)
         xs_all = tile(WIDE, U8, "xs_all")
@@ -99,8 +101,8 @@ def tile_moe_dyn_silu_kernel(
         def permute_scales(j, blocks):
             t = tile(blocks * H, U8, "w1p%d" % j)
             nc.vector.tensor_copy(
-                t[:].rearrange("p (m t c) -> p m t c", m=blocks, t=PACK),
-                w1s[j][:, : blocks * H].rearrange("p (m c t) -> p m t c", m=blocks, t=PACK),
+                t[:].rearrange("p (m t h c) -> p m h t c", m=blocks, t=PACK, c=LINE),
+                w1s[j][:, : blocks * H].rearrange("p (m h c t) -> p m h t c", m=blocks, t=PACK, c=LINE),
             )
             return t
 

@@ -35,7 +35,7 @@ def tile_moe_dyn_silu_kernel(
         psum = ctx.enter_context(tc.psum_pool(name="psum", bufs=1))
 
         def tile(width, dtype, name, over=""):
-            return keep.tile([P, width], dtype, name=name, tag=over or name, align_bytes=64)
+            return keep.tile([P, width], dtype, name=name, tag=over or name, align_bytes=256)
 
         def words_of(src):
             return src[0].rearrange("p c d -> p (c d)").bitcast(I32)
@@ -95,8 +95,8 @@ def tile_moe_dyn_silu_kernel(
         nc.sync.dma_start(g[:], gate)
 
         hT, quantised, w2w = {}, {}, {}
-        y = keep.tile([P, HALVES, T], F32, name="y")
-        res = [keep.tile([P, T], F32, name="res%d" % a) for a in range(HALVES)]
+        y = [tile(T, F32, "y%d" % a) for a in range(HALVES)]
+        res = [tile(T, F32, "res%d" % a) for a in range(HALVES)]
 
         def permute_scales(j, blocks):
             t = tile(blocks * H, U8, "w1p%d" % j)
@@ -186,15 +186,14 @@ def tile_moe_dyn_silu_kernel(
             return psum.tile([P, HALVES, S], F32, name=name, tag=tag)
 
         def times_gate(acc, a, lo, hi):
-            nc.vector.tensor_tensor(y[:, a, lo:hi], acc, g[:, lo:hi], mybir.AluOpType.mult)
+            nc.vector.tensor_tensor(y[a][:, lo:hi], acc, g[:, lo:hi], mybir.AluOpType.mult)
 
-        def scatter(a, first, last, on_scalar):
-            lo, hi = S * first, S * last + S
+        def scatter(a, lo, hi, on_scalar):
             window = res[a][:].indirect(entries(tok, lo, hi))
             if on_scalar:
-                nc.scalar.activation(window, y[:, a, lo:hi], mybir.ActivationFunctionType.Copy)
+                nc.scalar.activation(window, y[a][:, lo:hi], mybir.ActivationFunctionType.Copy)
             else:
-                nc.vector.tensor_copy(window, y[:, a, lo:hi])
+                nc.vector.tensor_copy(window, y[a][:, lo:hi])
 
         w2s_staged = gather_scales(w2s_all, col2, 0, B * N, "w2s_staged")
         xw = gather_words(xw_all, tok, 0, T, "xw")
@@ -206,44 +205,39 @@ def tile_moe_dyn_silu_kernel(
         w1p = [permute_scales(0, 2), permute_scales(1, 1)]
         xs = gather_scales(xs_all, tok, 0, T, "xs")
 
+        def second_words(m, over=""):
+            w2w[m] = gather_words(w2w_all, col2, N * m, N * m + N, "w2w%d" % m, over)
+
         first_layer(0)
         hs3 = first_layer_turned(3)
         first_layer(1)
         first_layer(2)
         turn(3, hs3)
-        def second_words(m):
-            w2w[m] = gather_words(w2w_all, col2, N * m, N * m + N, "w2w%d" % m, "w2w%d" % (m % 3))
-
         quantise(0)
         for m in range(B - 1):
             second_words(m)
         quantise(1)
-        for a in range(HALVES):
-            acc = bank("acc0_%d" % a, "acc0_%d" % a)
-            second_product(0, a, acc[:, 0, :])
-            times_gate(acc[:, 0, :], a, 0, S)
-        second_words(3)
+        lower0, upper, lower1 = bank("lower0", "lower0"), bank("upper", "upper"), bank("lower1", "lower0")
+        second_product(0, 0, lower0[:, 0, :])
+        second_product(0, 1, upper[:, 0, :])
+        second_product(1, 1, upper[:, 1, :])
+        times_gate(lower0[:, 0, :], 0, 0, S)
+        second_product(1, 0, lower1[:, 0, :])
+        second_words(3, over="w2w0")
         quantise(2)
-        acc = bank("acc1", "acc1")
-        for a in range(HALVES):
-            second_product(1, a, acc[:, a, :])
-        nc.vector.tensor_tensor(
-            y[:, :, S : 2 * S],
-            acc[:],
-            g[:, S : 2 * S].unsqueeze(1).to_broadcast([P, HALVES, S]),
-            mybir.AluOpType.mult,
-        )
+        times_gate(upper[:].rearrange("p m s -> p (m s)"), 1, 0, 2 * S)
+        times_gate(lower1[:, 0, :], 0, S, 2 * S)
         quantise(3)
+        scatter(0, 0, S, True)
+        scatter(0, S, 2 * S, False)
         late = [bank("late0", "pre1"), bank("late1", "pre0")]
         for m in (2, 3):
             for a in range(HALVES):
                 second_product(m, a, late[a][:, m - 2, :])
         for a in range(HALVES):
             times_gate(late[a][:].rearrange("p m s -> p (m s)"), a, 2 * S, B * S)
-        scatter(0, 0, 0, True)
-        scatter(1, 0, 1, True)
-        scatter(1, 2, 3, True)
-        scatter(0, 1, 1, False)
-        scatter(0, 2, 3, False)
+        scatter(1, 0, 2 * S, True)
+        scatter(1, 2 * S, T, True)
+        scatter(0, 2 * S, T, False)
         for a in range(HALVES):
             nc.sync.dma_start(out[P * a : P * a + P, :], res[a][:])

@@ -67,6 +67,9 @@ def tile_moe_dyn_silu_kernel(
             nc.vector.tensor_copy(t[:], table[:].indirect(entries(lst, a, b)))
             return t
 
+        ident = keep.tile([P, P], F32, name="ident")
+        nc.vector.memset(ident[:], 0.0)
+        make_identity(nc, ident[:], nomemset=True)
         w1s_all = tile(E * H, U8, "w1s_all")
         nc.gpsimd.memset(w1s_all[:, : E * H // 2].bitcast(I32), 0)
         nc.vector.memset(w1s_all[:, E * H // 2 :].bitcast(I32), 0)
@@ -76,9 +79,6 @@ def tile_moe_dyn_silu_kernel(
         nc.vector.memset(w2s[:].bitcast(I32), 0)
         xs_all = tile(WIDE, U8, "xs_all")
         nc.vector.memset(xs_all[:].bitcast(I32), 0)
-        ident = keep.tile([P, P], F32, name="ident")
-        nc.vector.memset(ident[:], 0.0)
-        make_identity(nc, ident[:], nomemset=True)
 
         col2 = load_list(offs3, "col2")
         nc.scalar.dma_start(w2s_all[STAGE:, :].bitcast(I32), w2_scales[0].bitcast(I32))

from contextlib import ExitStack

import concourse.mybir as mybir
from concourse.masks import make_identity

K, T, E, B, H, N = 512, 512, 8, 4, 512, 256
FLOPS = 2 * 128 * B * (K * H + H * N)

F32 = mybir.dt.float32
BF16 = mybir.dt.bfloat16
I32 = mybir.dt.int32
U32 = mybir.dt.uint32
U16 = mybir.dt.uint16
U8 = mybir.dt.uint8
FP8X4 = mybir.dt.float8_e4m3fn_x4

P = 128
S = 128
PACK = 4
LIST = 16
WIDE = T + 192
HALVES = N // P
X_ROW, W1_ROW, W2_ROW = 0, 4, 8
STAGE = P - 16
LINE = 16
AHEAD = 2


def tile_moe_dyn_silu_kernel(
    tc, x_words, x_scales, w1_words, w1_scales, w2_words, w2_scales, gate, offs, offs2, offs3, out
):
    nc = tc.nc
    with ExitStack() as ctx:
        keep = ctx.enter_context(tc.tile_pool(name="keep", bufs=1))
        psum = ctx.enter_context(tc.psum_pool(name="psum", bufs=1))

        def tile(width, dtype, name, over=""):
            return keep.tile([P, width], dtype, name=name, tag=over or name, align_bytes=256)

        def words_of(src):
            return src[0].rearrange("p c d -> p (c d)").bitcast(I32)

        def load_list(src, name):
            t = keep.tile([P, src.shape[1]], U16, name=name)
            nc.sync.dma_start(t[:], src)
            return t

        def load_words(src, name, width, over=""):
            t = tile(width, I32, name, over)
            nc.sync.dma_start(t[:, : src.shape[2]], words_of(src))
            return t

        def load_scales(t, src, row):
            for q in range(4):
                nc.sync.dma_start(t[row + q : P : 32, : src.shape[2]].bitcast(I32), src[0, q:16:4, :].bitcast(I32))

        def entries(lst, a, b):
            return lst[:, a // LIST : b // LIST]

        def gather_words(table, lst, a, b, name, over=""):
            t = tile(b - a, I32, name, over)
            nc.vector.tensor_copy(t[:].bitcast(U32), table[:].bitcast(U32).indirect(entries(lst, a, b)))
            return t

        def gather_scales(table, lst, a, b, name):
            t = tile(b - a, U8, name)
            nc.vector.tensor_copy(t[:], table[:].indirect(entries(lst, a, b)))
            return t

        ident = keep.tile([P, P], F32, name="ident")
        nc.vector.memset(ident[:], 0.0)
        make_identity(nc, ident[:], nomemset=True)
        w1s_all = tile(E * H, U8, "w1s_all")
        nc.gpsimd.memset(w1s_all[:, : E * H // 2].bitcast(I32), 0)
        nc.vector.memset(w1s_all[:, E * H // 2 :].bitcast(I32), 0)
        w2s_all = tile(E * N, U8, "w2s_all")
        nc.vector.memset(w2s_all[:STAGE, :].bitcast(I32), 0)
        w2s = tile(B * N, U8, "w2s")
        nc.vector.memset(w2s[:].bitcast(I32), 0)
        xs_all = tile(WIDE, U8, "xs_all")
        nc.vector.memset(xs_all[:].bitcast(I32), 0)

        col2 = load_list(offs3, "col2")
        nc.scalar.dma_start(w2s_all[STAGE:, :].bitcast(I32), w2_scales[0].bitcast(I32))
        tok = load_list(offs, "tok")
        xw_all = load_words(x_words, "xw_all", WIDE)
        load_scales(w1s_all, w1_scales, W1_ROW)
        col1 = load_list(offs2, "col1")
        w1w_all = tile(E * H, I32, "w1w_all")
        half = E * H // 2
        nc.sync.dma_start(w1w_all[:, :half], words_of(w1_words)[:, :half])
        load_scales(xs_all, x_scales, X_ROW)
        nc.sync.dma_start(w1w_all[:, half:], words_of(w1_words)[:, half:])
        g = tile(S * B, F32, "g")
        nc.sync.dma_start(g[:], gate)

        hT, quantised, w2w = {}, {}, {}
        y = [tile(T, F32, "y%d" % a) for a in range(HALVES)]
        res = [tile(T, F32, "res%d" % a) for a in range(HALVES)]

        def permute_scales(j, blocks):
            t = tile(blocks * H, U8, "w1p%d" % j)
            nc.vector.tensor_copy(
                t[:].rearrange("p (m t h c) -> p m h t c", m=blocks, t=PACK, c=LINE),
                w1s[j][:, : blocks * H].rearrange("p (m h c t) -> p m h t c", m=blocks, t=PACK, c=LINE),
            )
            return t

        def first_layer_turned(m):
            w1w = gather_words(w1w_all, col1, H * m, H * m + H, "w1w%d" % m)
            cols = slice(S * m, S * m + S)
            pre = psum.tile([P, H], F32, name="pre%d" % m, tag="pre%d" % m)
            nc.tensor.matmul_mx(
                out=pre[:],
                lhsT=xw[:, cols].bitcast(FP8X4),
                lhsT_scale=xs[X_ROW:, cols],
                rhs=w1w[:].bitcast(FP8X4),
                rhs_scale=w1s[m // 2][W1_ROW:, H * (m % 2) : H * (m % 2) + H],
                start=True,
                stop=True,
            )
            hs = tile(H, BF16, "hs")
            nc.scalar.activation(
                hs[:].rearrange("s (v p e) -> s v p e", v=2, e=2),
                pre[:].rearrange("s (p v e) -> s v p e", v=2, e=2),
                mybir.ActivationFunctionType.Silu,
            )
            return hs

        def turn(m, hs):
            turned = psum.tile([P, 2, S], F32, name="turned")
            for v in range(2):
                nc.tensor.transpose(turned[:, v, :], hs[:].bitcast(F32)[:, P * v : P * v + P], ident[:])
            hT[m] = tile(PACK * S, BF16, "hT%d" % m)
            nc.scalar.copy(
                hT[m][:].bitcast(F32).rearrange("p (s v) -> p s v", v=2),
                turned[:].rearrange("p v s -> p s v"),
            )

        def first_layer(m):
            w1w = tile(H, I32, "w1w%d" % m)
            nc.vector.tensor_copy(
                w1w[:].bitcast(U32).rearrange("p (t c) -> p c t", t=PACK),
                w1w_all[:].bitcast(U32).indirect(entries(col1, H * m, H * m + H)),
            )
            cols = slice(S * m, S * m + S)
            pre = psum.tile([P, PACK, S], F32, name="pre%d" % m, tag="pre%d" % m)
            for t in range(PACK):
                c = H * (m % 2) + P * t
                nc.tensor.matmul_mx(
                    out=pre[:, t, :],
                    lhsT=w1w[:, P * t : P * t + P].bitcast(FP8X4),
                    lhsT_scale=w1p[m // 2][W1_ROW:, c : c + P],
                    rhs=xw[:, cols].bitcast(FP8X4),
                    rhs_scale=xs[X_ROW:, cols],
                    start=True,
                    stop=True,
                )
            hT[m] = tile(PACK * S, BF16, "hT%d" % m)
            nc.scalar.activation(
                hT[m][:].rearrange("p (s t) -> p s t", t=PACK),
                pre[:].rearrange("p t s -> p s t"),
                mybir.ActivationFunctionType.Silu,
            )

        def quantise(m):
            hq = tile(S, I32, "hq%d" % m, "hq%d" % (m % 2))
            hqs = tile(S, U8, "hqs%d" % m)
            nc.vector.quantize_mx(out=hq[:].bitcast(FP8X4), scales=hqs[:], in_=hT[m][:])
            quantised[m] = hq, hqs

        def second_product(m, a, acc):
            hq, hqs = quantised[m]
            c = N * m + P * a
            nc.tensor.matmul_mx(
                out=acc,
                lhsT=w2w[m][:, P * a : P * a + P].bitcast(FP8X4),
                lhsT_scale=w2s[W2_ROW:, c : c + P],
                rhs=hq[:].bitcast(FP8X4),
                rhs_scale=hqs[:],
                start=True,
                stop=True,
            )

        def bank(name, tag):
            return psum.tile([P, HALVES, S], F32, name=name, tag=tag)

        def times_gate(acc, a, lo, hi):
            nc.vector.tensor_tensor(y[a][:, lo:hi], acc, g[:, lo:hi], mybir.AluOpType.mult)

        def scatter(a, lo, hi, on_scalar):
            window = res[a][:].indirect(entries(tok, lo, hi))
            if on_scalar:
                nc.scalar.activation(window, y[a][:, lo:hi], mybir.ActivationFunctionType.Copy)
            else:
                nc.vector.tensor_copy(window, y[a][:, lo:hi])

        w2s_staged = gather_scales(w2s_all, col2, 0, B * N, "w2s_staged")
        xw = gather_words(xw_all, tok, 0, T, "xw")
        for q in range(4):
            if q == AHEAD:
                w2w_all = load_words(w2_words, "w2w_all", E * N, over="w2s_all")
            nc.sync.dma_start(w2s[W2_ROW + q : P : 32, :].bitcast(I32), w2s_staged[STAGE + q : P : 4, :].bitcast(I32))
        w1s = [gather_scales(w1s_all, col1, 2 * H * j, 2 * H * j + 2 * H, "w1s%d" % j) for j in range(2)]
        w1p = [permute_scales(0, 2), permute_scales(1, 1)]
        xs = gather_scales(xs_all, tok, 0, T, "xs")

        def second_words(m, over=""):
            w2w[m] = gather_words(w2w_all, col2, N * m, N * m + N, "w2w%d" % m, over)

        first_layer(0)
        hs3 = first_layer_turned(3)
        first_layer(1)
        first_layer(2)
        turn(3, hs3)
        quantise(0)
        for m in range(B - 1):
            second_words(m)
        quantise(1)
        lower0, upper, lower1 = bank("lower0", "lower0"), bank("upper", "upper"), bank("lower1", "lower0")
        second_product(0, 0, lower0[:, 0, :])
        second_product(0, 1, upper[:, 0, :])
        second_product(1, 1, upper[:, 1, :])
        times_gate(lower0[:, 0, :], 0, 0, S)
        second_product(1, 0, lower1[:, 0, :])
        second_words(3, over="w2w0")
        quantise(2)
        times_gate(upper[:].rearrange("p m s -> p (m s)"), 1, 0, 2 * S)
        times_gate(lower1[:, 0, :], 0, S, 2 * S)
        quantise(3)
        scatter(0, 0, S, True)
        scatter(0, S, 2 * S, False)
        late = [bank("late0", "pre1"), bank("late1", "pre0")]
        for m in (2, 3):
            for a in range(HALVES):
                second_product(m, a, late[a][:, m - 2, :])
        for a in range(HALVES):
            times_gate(late[a][:].rearrange("p m s -> p (m s)"), a, 2 * S, B * S)
        scatter(1, 0, 2 * S, True)
        scatter(1, 2 * S, T, True)
        scatter(0, 2 * S, T, False)
        for a in range(HALVES):
            nc.sync.dma_start(out[P * a : P * a + P, :], res[a][:])
